import numpy as np
import ml_dtypes


def mxq(x, axis, fmt="e4m3"):
    dtype, down = {"e4m3": (ml_dtypes.float8_e4m3fn, 7), "e5m2": (ml_dtypes.float8_e5m2, 14)}[fmt]
    v = np.moveaxis(np.asarray(x, np.float32).astype(ml_dtypes.bfloat16).astype(np.float64), axis, -1)
    blocks = v.reshape(v.shape[:-1] + (-1, 32))
    amax = np.abs(blocks).max(-1, keepdims=True)
    byte = np.maximum(np.where(amax > 0, np.frexp(amax)[1] - 1 + 127, 0) - down, 1)
    scale = np.exp2(byte - 127.0)
    codes = (blocks / scale).astype(np.float32).astype(dtype).astype(np.float64)
    return np.moveaxis((codes * scale).reshape(v.shape), -1, axis)


WIDE = False


def mx_kscale(k):
    if not WIDE:
        return np.ones(k)
    levels = np.array([10, -10, 5, -5, 0])
    if k % 512:
        return np.exp2(np.random.permutation(np.resize(levels, k // 32))).repeat(32)
    a = np.empty((k // 512, 16))
    for p in range(k // 512):
        a[p, :8] = np.random.permutation(np.resize(levels, 8))
        for g in range(8):
            far = levels[np.abs(levels - a[p, g]) >= 10]
            a[p, g + 8] = far[np.random.randint(len(far))]
    return np.exp2(a.ravel()).repeat(32)


def f64(x):
    return np.asarray(x).astype(np.float64)


def striped(idx):
    return np.tile(idx.reshape(-1, 16).T, (8, 1)).astype(np.uint16)


def unstriped(offs):
    return offs[:16].T.reshape(-1).astype(np.int64)


E2M1 = np.array([0.0, 0.5, 1.0, 1.5, 2.0, 3.0, 4.0, 6.0, -0.0, -0.5, -1.0, -1.5, -2.0, -3.0, -4.0, -6.0])


def pack_weight(w, fmt):
    k, n = w.shape
    w = f64(np.asarray(w, np.float32).astype(ml_dtypes.bfloat16)).reshape(k // 32, 32, n)
    amax = np.abs(w).max(1)
    if fmt == "e4m3":
        byte = np.frexp(amax)[1] - 1 + 127 - 7
    else:
        mant, ex = np.frexp(amax / 6.0)
        byte = np.where(mant > 0.5, ex, ex - 1) + 127
    byte = np.clip(np.where(amax > 0, byte, 1), 1, 254)
    scaled = (w * np.exp2(127.0 - byte)[:, None, :]).reshape(k, n).astype(np.float32)
    by_word = np.ascontiguousarray(scaled.reshape(k // 512, 128, 4, n).transpose(0, 1, 3, 2))
    if fmt == "e4m3":
        words = by_word.astype(ml_dtypes.float8_e4m3fn).view(np.uint8)
    else:
        c = by_word.astype(ml_dtypes.float4_e2m1fn).view(np.uint8) & 0xF
        words = (c[..., 0::2] | (c[..., 1::2] << 4)).reshape(k // 512, 128, 2 * n)
    return np.ascontiguousarray(words), np.ascontiguousarray(byte.astype(np.uint8).reshape(k // 512, 16, n))


def unpack_weight(words, scales, fmt):
    g, _, n = scales.shape
    words = np.ascontiguousarray(words).reshape(g, 128, n, -1)
    if fmt == "e4m3":
        vals = words.view(ml_dtypes.float8_e4m3fn).astype(np.float64)
    else:
        nib = np.empty((g, 128, n, 4), np.uint8)
        nib[..., 0::2] = words & 0xF
        nib[..., 1::2] = words >> 4
        vals = E2M1[nib]
    vals = vals * np.repeat(np.exp2(scales.astype(np.float64) - 127.0), 8, axis=1)[..., None]
    return vals.transpose(0, 1, 3, 2).reshape(g * 512, n)


def pack_table(v):
    words, scales = pack_weight(v, "e4m3")
    return np.concatenate([words.reshape(words.shape[0], -1), scales.reshape(scales.shape[0], -1)], axis=1)


def unpack_table(tab):
    g, t = tab.shape[0], tab.shape[1] // 528
    return unpack_weight(tab[:, :512 * t].reshape(g, 128, t, 4), tab[:, 512 * t:].reshape(g, 16, t), "e4m3")


K, M, T, S = 1024, 512, 512, 256


def setup_inputs():
    n = np.random.standard_normal
    s = mx_kscale(K)[:, None]
    return {
        "tab": pack_table(n((K, T)) * s),
        "w": (n((K, M)) / np.sqrt(K) / s).astype(np.float32),
        "offs": striped(np.random.permutation(T)[:S]),
    }


def reference(tab, w, offs):
    tab_ = unpack_table(tab)[:, unstriped(offs)]
    w_ = mxq(f64(w), 0, "e4m3")
    y = w_.T @ tab_
    return y

@@ -1,0 +1,125 @@
+from contextlib import ExitStack
+
+import concourse.mybir as mybir
+
+K, M, T, S = 1024, 512, 512, 256
+FLOPS = 2 * K * M * S
+
+F32 = mybir.dt.float32
+BF16 = mybir.dt.bfloat16
+I32 = mybir.dt.int32
+U32 = mybir.dt.uint32
+U16 = mybir.dt.uint16
+U8 = mybir.dt.uint8
+FP8X4 = mybir.dt.float8_e4m3fn_x4
+
+P = 128
+PACK = 4
+PASSES = K // (P * PACK)
+M_TILE = 128
+CHUNKS = (
+    (0, 0, 256, ((0, 256, 112),)),
+    (1, 0, 256, ((0, 256, 112),)),
+    (0, 256, 512, ((0, 256, 112),)),
+    (1, 256, 384, ((0, 128, 64),)),
+    (1, 384, 512, ((0, 128, 72),)),
+)
+PARTS = (((0, S, "scalar"),), ((0, S, "scalar"),), ((0, S, "scalar"),), ((0, 128, "scalar"), (128, S, "vector")))
+
+
+def interleave(copy, grouped, raw, first, last):
+    copy(
+        out=grouped[:, first:last, :].rearrange("p (c i) t -> p c t i", i=4),
+        in_=raw[:, :, first:last].rearrange("p t (c i) -> p c t i", i=4),
+    )
+
+
+def tile_list_tabw_none_kernel(tc, tab, w, offs, out):
+    nc = tc.nc
+    with ExitStack() as ctx:
+        held = ctx.enter_context(tc.tile_pool(name="held", bufs=1))
+        psum = ctx.enter_context(tc.psum_pool(name="psum", bufs=1))
+
+        offsets = held.tile([P, S // 16], U16, name="offsets")
+        nc.sync.dma_start(offsets[:], offs)
+
+        tab_words = tab.bitcast(I32)
+        row = T // 4
+        w_rows = w.rearrange("(a p j) m -> a p j m", p=P, j=PACK)
+
+        def load_words(a):
+            tile = held.tile([P, T], I32, name=f"words{a}", align_bytes=64)
+            nc.sync.dma_start(tile[:], tab_words[a, 0 : P * T].rearrange("(p t) -> p t", p=P))
+            return tile
+
+        def load_chunk(i):
+            a, first, last, pieces = CHUNKS[i]
+            tile = held.tile([P, PACK, last - first], F32, name=f"raw{i}", align_bytes=64)
+            nc.sync.dma_start(tile[:], w_rows[a][:, :, first:last])
+            return tile
+
+        def pick(a, words):
+            tile = held.tile([P, S], U32, name=f"picked{a}", align_bytes=64)
+            nc.vector.tensor_copy(tile[:], words[:].bitcast(U32).indirect(offsets[:]))
+            return tile
+
+        tab_scales = held.tile([P, T // 4], I32, name="tab_scales", align_bytes=64)
+        nc.vector.memset(tab_scales[:], 0)
+        words = {}
+        raws = {}
+        picked = {}
+        words[0] = load_words(0)
+        for q in range(4):
+            rows = tab_words[:, P * T + 4 * q * row : P * T + 4 * (q + 1) * row]
+            nc.sync.dma_start(tab_scales[32 * q : 32 * q + 8, :], rows.rearrange("a (r t) -> a r t", r=4))
+        raws[0] = load_chunk(0)
+        words[1] = load_words(1)
+        raws[1] = load_chunk(1)
+        raws[2] = load_chunk(2)
+        raws[3] = load_chunk(3)
+        raws[4] = load_chunk(4)
+
+        picked[0] = pick(0, words[0])
+        picked_scales = held.tile([P, S], U8, name="picked_scales", align_bytes=64)
+        nc.vector.tensor_copy(picked_scales[:], tab_scales[:].bitcast(U8).indirect(offsets[:]))
+        sums = {}
+        for c, (a, first, last, pieces) in enumerate(CHUNKS):
+            raw = raws[c]
+            width = last - first
+            grouped = held.tile([P, width, PACK], BF16, name=f"grouped{c}", align_bytes=64)
+            codes = held.tile([P, width], U32, name=f"codes{c}", align_bytes=64)
+            plane = held.tile([P, width], U8, name=f"plane{c}", align_bytes=64)
+            for begin, end, share in pieces:
+                interleave(nc.vector.tensor_copy, grouped, raw, begin, begin + share)
+                interleave(nc.scalar.copy, grouped, raw, begin + share, end)
+            if c == 0:
+                picked[1] = pick(1, words[1])
+            for begin, end, share in pieces:
+                nc.vector.quantize_mx(
+                    out=codes[:, begin:end].bitcast(FP8X4),
+                    scales=plane[:, begin:end],
+                    in_=grouped[:, begin:end, :].rearrange("p w j -> p (w j)"),
+                )
+            for m in range(first // M_TILE, last // M_TILE):
+                cols = slice(m * M_TILE - first, (m + 1) * M_TILE - first)
+                for begin, end, copy in PARTS[m]:
+                    if a == 0:
+                        sums[m, begin] = psum.tile([M_TILE, end - begin], F32, name=f"sum{m}_{begin}")
+                    nc.tensor.matmul_mx(
+                        out=sums[m, begin][:],
+                        lhsT=codes[:, cols].bitcast(FP8X4),
+                        lhsT_scale=plane[:, cols],
+                        rhs=picked[a][:, begin:end].bitcast(FP8X4),
+                        rhs_scale=picked_scales[4 * a :, begin:end],
+                        start=(a == 0),
+                        stop=(a == PASSES - 1),
+                    )
+            if a == PASSES - 1:
+                for m in range(first // M_TILE, last // M_TILE):
+                    result = held.tile([M_TILE, S], F32, name=f"result{m}")
+                    for begin, end, copy in PARTS[m]:
+                        if copy == "vector":
+                            nc.vector.tensor_copy(out=result[:, begin:end], in_=sums[m, begin][:])
+                        else:
+                            nc.scalar.copy(out=result[:, begin:end], in_=sums[m, begin][:])
+                    nc.sync.dma_start(out=out[m * M_TILE : (m + 1) * M_TILE, :], in_=result[:])

@@ -18,13 +18,16 @@ PACK = 4
 PASSES = K // (P * PACK)
 M_TILE = 128
 CHUNKS = (
-    (0, 0, 256, ((0, 256, 112),)),
-    (1, 0, 256, ((0, 256, 112),)),
-    (0, 256, 512, ((0, 256, 112),)),
-    (1, 256, 384, ((0, 128, 64),)),
-    (1, 384, 512, ((0, 128, 72),)),
+    (0, 0, 256, 96),
+    (1, 0, 256, 128),
+    (0, 256, 384, 64),
+    (1, 256, 384, 64),
+    (0, 384, 512, 64),
+    (1, 384, 512, 64),
 )
-PARTS = (((0, S, "scalar"),), ((0, S, "scalar"),), ((0, S, "scalar"),), ((0, 128, "scalar"), (128, S, "vector")))
+PLACES = ((64, True), (384, True), (0, False), (320, False), (64, True), (384, True))
+RESULT_ON = (3, 5, None, None)
+PARTS = (((0, S, "scalar", "sync"),), ((0, S, "scalar", "sync"),), ((0, S, "scalar", "sync"),), ((0, 128, "vector", "none"), (128, S, "scalar", "sync")))
 
 
 def interleave(copy, grouped, raw, first, last):
@@ -41,85 +44,141 @@ def tile_list_tabw_none_kernel(tc, tab, w, offs, out):
         psum = ctx.enter_context(tc.psum_pool(name="psum", bufs=1))
 
         offsets = held.tile([P, S // 16], U16, name="offsets")
-        nc.sync.dma_start(offsets[:], offs)
-
         tab_words = tab.bitcast(I32)
         row = T // 4
         w_rows = w.rearrange("(a p j) m -> a p j m", p=P, j=PACK)
-
-        def load_words(a):
-            tile = held.tile([P, T], I32, name=f"words{a}", align_bytes=64)
-            nc.sync.dma_start(tile[:], tab_words[a, 0 : P * T].rearrange("(p t) -> p t", p=P))
-            return tile
-
-        def load_chunk(i):
-            a, first, last, pieces = CHUNKS[i]
-            tile = held.tile([P, PACK, last - first], F32, name=f"raw{i}", align_bytes=64)
-            nc.sync.dma_start(tile[:], w_rows[a][:, :, first:last])
-            return tile
-
-        def pick(a, words):
-            tile = held.tile([P, S], U32, name=f"picked{a}", align_bytes=64)
-            nc.vector.tensor_copy(tile[:], words[:].bitcast(U32).indirect(offsets[:]))
-            return tile
-
-        tab_scales = held.tile([P, T // 4], I32, name="tab_scales", align_bytes=64)
-        nc.vector.memset(tab_scales[:], 0)
         words = {}
         raws = {}
         picked = {}
-        words[0] = load_words(0)
-        for q in range(4):
-            rows = tab_words[:, P * T + 4 * q * row : P * T + 4 * (q + 1) * row]
-            nc.sync.dma_start(tab_scales[32 * q : 32 * q + 8, :], rows.rearrange("a (r t) -> a r t", r=4))
-        raws[0] = load_chunk(0)
-        words[1] = load_words(1)
-        raws[1] = load_chunk(1)
-        raws[2] = load_chunk(2)
-        raws[3] = load_chunk(3)
-        raws[4] = load_chunk(4)
-
-        picked[0] = pick(0, words[0])
-        picked_scales = held.tile([P, S], U8, name="picked_scales", align_bytes=64)
-        nc.vector.tensor_copy(picked_scales[:], tab_scales[:].bitcast(U8).indirect(offsets[:]))
+        codes = {}
+        planes = {}
+        grouped = {}
         sums = {}
-        for c, (a, first, last, pieces) in enumerate(CHUNKS):
-            raw = raws[c]
+        tab_scales = held.tile([P, T // 4], I32, name="tab_scales", align_bytes=64)
+        picked_scales = held.tile([P, S], U8, name="picked_scales", align_bytes=64)
+
+        ring = held.tile([P, 640, PACK], BF16, name="ring", align_bytes=64)
+
+        def load_words(a):
+            words[a] = held.tile([P, T], I32, name=f"words{a}", align_bytes=64)[:]
+            nc.sync.dma_start(words[a], tab_words[a, 0 : P * T].rearrange("(p t) -> p t", p=P))
+
+        def load_both_words():
+            both = held.tile([P, PASSES, T], I32, name="words", align_bytes=64)
+            nc.sync.dma_start(both[:], tab_words[:, 0 : P * T].rearrange("a (p t) -> p a t", p=P))
+            for a in range(PASSES):
+                words[a] = both[:, a, :]
+
+        def load_scales(q, queue):
+            rows = tab_words[:, P * T + 4 * q * row : P * T + 4 * (q + 1) * row]
+            queue.dma_start(tab_scales[32 * q : 32 * q + 8, :], rows.rearrange("a (r t) -> a r t", r=4))
+
+        def load_chunk(c):
+            a, first, last, share = CHUNKS[c]
+            raws[c] = held.tile([P, PACK, last - first], F32, name=f"raw{c}", align_bytes=64)
+            nc.sync.dma_start(raws[c][:], w_rows[a][:, :, first:last])
+
+        def pick(a):
+            picked[a] = held.tile([P, S], U32, name=f"picked{a}", align_bytes=64)
+            nc.vector.tensor_copy(picked[a][:], words[a].bitcast(U32).indirect(offsets[:]))
+
+        def pick_scales():
+            nc.vector.tensor_copy(picked_scales[:], tab_scales[:].bitcast(U8).indirect(offsets[:]))
+
+        def weave(c):
+            a, first, last, share = CHUNKS[c]
             width = last - first
-            grouped = held.tile([P, width, PACK], BF16, name=f"grouped{c}", align_bytes=64)
-            codes = held.tile([P, width], U32, name=f"codes{c}", align_bytes=64)
-            plane = held.tile([P, width], U8, name=f"plane{c}", align_bytes=64)
-            for begin, end, share in pieces:
-                interleave(nc.vector.tensor_copy, grouped, raw, begin, begin + share)
-                interleave(nc.scalar.copy, grouped, raw, begin + share, end)
-            if c == 0:
-                picked[1] = pick(1, words[1])
-            for begin, end, share in pieces:
-                nc.vector.quantize_mx(
-                    out=codes[:, begin:end].bitcast(FP8X4),
-                    scales=plane[:, begin:end],
-                    in_=grouped[:, begin:end, :].rearrange("p w j -> p (w j)"),
-                )
+            start, vector_first = PLACES[c]
+            grouped[c] = ring[:, start : start + width, :]
+            cut = share if vector_first else width - share
+            engines = (nc.vector.tensor_copy, nc.scalar.copy) if vector_first else (nc.scalar.copy, nc.vector.tensor_copy)
+            if cut > 0:
+                interleave(engines[0], grouped[c], raws[c], 0, cut)
+            if cut < width:
+                interleave(engines[1], grouped[c], raws[c], cut, width)
+
+        def quantize(c):
+            a, first, last, share = CHUNKS[c]
+            width = last - first
+            codes[c] = held.tile([P, width], U32, name=f"codes{c}", align_bytes=64)
+            planes[c] = held.tile([P, width], U8, name=f"plane{c}", align_bytes=64)
+            nc.vector.quantize_mx(
+                out=codes[c][:].bitcast(FP8X4),
+                scales=planes[c][:],
+                in_=grouped[c].rearrange("p w j -> p (w j)"),
+            )
+
+        def multiply(c):
+            a, first, last, share = CHUNKS[c]
             for m in range(first // M_TILE, last // M_TILE):
                 cols = slice(m * M_TILE - first, (m + 1) * M_TILE - first)
-                for begin, end, copy in PARTS[m]:
-                    if a == 0:
+                for begin, end, copy, queue in PARTS[m]:
+                    opens = (m, begin) not in sums
+                    if opens:
                         sums[m, begin] = psum.tile([M_TILE, end - begin], F32, name=f"sum{m}_{begin}")
                     nc.tensor.matmul_mx(
                         out=sums[m, begin][:],
-                        lhsT=codes[:, cols].bitcast(FP8X4),
-                        lhsT_scale=plane[:, cols],
+                        lhsT=codes[c][:, cols].bitcast(FP8X4),
+                        lhsT_scale=planes[c][:, cols],
                         rhs=picked[a][:, begin:end].bitcast(FP8X4),
                         rhs_scale=picked_scales[4 * a :, begin:end],
-                        start=(a == 0),
-                        stop=(a == PASSES - 1),
+                        start=opens,
+                        stop=not opens,
                     )
-            if a == PASSES - 1:
-                for m in range(first // M_TILE, last // M_TILE):
-                    result = held.tile([M_TILE, S], F32, name=f"result{m}")
-                    for begin, end, copy in PARTS[m]:
-                        if copy == "vector":
-                            nc.vector.tensor_copy(out=result[:, begin:end], in_=sums[m, begin][:])
-                        else:
-                            nc.scalar.copy(out=result[:, begin:end], in_=sums[m, begin][:])
-                    nc.sync.dma_start(out=out[m * M_TILE : (m + 1) * M_TILE, :], in_=result[:])
+
+        def store(m):
+            if RESULT_ON[m] is None:
+                result = held.tile([M_TILE, S], F32, name=f"result{m}")[:]
+            else:
+                result = raws[RESULT_ON[m]][:].rearrange("p j c -> p (j c)")[:, 0:S]
+            done = 0
+            for begin, end, copy, queue in PARTS[m]:
+                if copy == "vector":
+                    nc.vector.tensor_copy(out=result[:, begin:end], in_=sums[m, begin][:])
+                else:
+                    nc.scalar.copy(out=result[:, begin:end], in_=sums[m, begin][:])
+                if queue == "sync":
+                    nc.sync.dma_start(out=out[m * M_TILE : (m + 1) * M_TILE, done:end], in_=result[:, done:end])
+                    done = end
+                if queue == "scalar":
+                    nc.scalar.dma_start(out=out[m * M_TILE : (m + 1) * M_TILE, done:end], in_=result[:, done:end])
+                    done = end
+
+        nc.vector.memset(tab_scales[:], 0)
+        load_both_words()
+        nc.sync.dma_start(offsets[:], offs)
+        load_scales(0, nc.sync)
+        load_scales(1, nc.sync)
+        load_scales(2, nc.sync)
+        load_scales(3, nc.sync)
+        load_chunk(0)
+        load_chunk(1)
+        load_chunk(2)
+        load_chunk(3)
+        load_chunk(4)
+        load_chunk(5)
+        pick(0)
+        pick(1)
+        pick_scales()
+        weave(0)
+        quantize(0)
+        multiply(0)
+        weave(1)
+        weave(2)
+        quantize(1)
+        multiply(1)
+        quantize(2)
+        multiply(2)
+        weave(3)
+        quantize(3)
+        multiply(3)
+        store(0)
+        weave(4)
+        quantize(4)
+        multiply(4)
+        weave(5)
+        quantize(5)
+        multiply(5)
+        store(1)
+        store(2)
+        store(3)

@@ -18,16 +18,18 @@ PACK = 4
 PASSES = K // (P * PACK)
 M_TILE = 128
 CHUNKS = (
-    (0, 0, 256, 96),
-    (1, 0, 256, 128),
-    (0, 256, 384, 64),
-    (1, 256, 384, 64),
-    (0, 384, 512, 64),
-    (1, 384, 512, 64),
+    (0, 0, 256, 0, 0),
+    (0, 256, 512, 0, 0),
+    (1, 0, 128, 128, 1),
+    (1, 128, 256, 0, 1),
+    (1, 256, 384, 64, 2),
+    (1, 384, 512, 80, 3),
 )
-PLACES = ((64, True), (384, True), (0, False), (320, False), (64, True), (384, True))
-RESULT_ON = (3, 5, None, None)
-PARTS = (((0, S, "scalar", "sync"),), ((0, S, "scalar", "sync"),), ((0, S, "scalar", "sync"),), ((0, 128, "vector", "none"), (128, S, "scalar", "sync")))
+PLACES = ((0, True), (256, True), (256, True), (512, True), (320, True), (None, True))
+RESULT_ON = (None, None, None, None)
+LOADS = ((0, 0, 512), (1, 0, 256), (1, 256, 384), (1, 384, 512))
+LAST_ON = 2
+PARTS = (((0, S, "scalar", "sync"),), ((0, S, "vector", "sync"),), ((0, S, "scalar", "sync"),), ((0, 128, "vector", "none"), (128, S, "scalar", "sync")))
 
 
 def interleave(copy, grouped, raw, first, last):
@@ -74,9 +76,21 @@ def tile_list_tabw_none_kernel(tc, tab, w, offs, out):
             queue.dma_start(tab_scales[32 * q : 32 * q + 8, :], rows.rearrange("a (r t) -> a r t", r=4))
 
         def load_chunk(c):
-            a, first, last, share = CHUNKS[c]
+            a, first, last = LOADS[c]
             raws[c] = held.tile([P, PACK, last - first], F32, name=f"raw{c}", align_bytes=64)
             nc.sync.dma_start(raws[c][:], w_rows[a][:, :, first:last])
+
+        def load_pair(u):
+            if u == 0:
+                raws[0] = held.tile([P, PACK, M], F32, name="raw0", align_bytes=64)
+            nc.sync.dma_start(raws[0][:, 2 * u : 2 * u + 2, :], w_rows[0][:, 2 * u : 2 * u + 2, :])
+
+        def weave_pair(copy, c, u, begin, end):
+            a, first, last, share, load = CHUNKS[c]
+            start, vector_first = PLACES[c]
+            grouped[c] = ring[:, start : start + last - first, :]
+            rows = slice(2 * u, 2 * u + 2)
+            interleave(copy, grouped[c][:, :, rows], raws[0][:, rows, first:last], begin, end)
 
         def pick(a):
             picked[a] = held.tile([P, S], U32, name=f"picked{a}", align_bytes=64)
@@ -86,21 +100,25 @@ def tile_list_tabw_none_kernel(tc, tab, w, offs, out):
             nc.vector.tensor_copy(picked_scales[:], tab_scales[:].bitcast(U8).indirect(offsets[:]))
 
         def weave(c):
-            a, first, last, share = CHUNKS[c]
+            a, first, last, share, load = CHUNKS[c]
             width = last - first
+            raw = raws[load][:, :, first - LOADS[load][1] : last - LOADS[load][1]]
             start, vector_first = PLACES[c]
-            grouped[c] = ring[:, start : start + width, :]
+            if start is None:
+                grouped[c] = held.tile([P, width, PACK], BF16, name=f"grouped{c}", tag=f"codes{LAST_ON}", align_bytes=64)[:]
+            else:
+                grouped[c] = ring[:, start : start + width, :]
             cut = share if vector_first else width - share
             engines = (nc.vector.tensor_copy, nc.scalar.copy) if vector_first else (nc.scalar.copy, nc.vector.tensor_copy)
             if cut > 0:
-                interleave(engines[0], grouped[c], raws[c], 0, cut)
+                interleave(engines[0], grouped[c], raw, 0, cut)
             if cut < width:
-                interleave(engines[1], grouped[c], raws[c], cut, width)
+                interleave(engines[1], grouped[c], raw, cut, width)
 
         def quantize(c):
-            a, first, last, share = CHUNKS[c]
+            a, first, last, share, load = CHUNKS[c]
             width = last - first
-            codes[c] = held.tile([P, width], U32, name=f"codes{c}", align_bytes=64)
+            codes[c] = held.tile([P, width], U32, name=f"codes{c}", tag=f"codes{c}", align_bytes=64)
             planes[c] = held.tile([P, width], U8, name=f"plane{c}", align_bytes=64)
             nc.vector.quantize_mx(
                 out=codes[c][:].bitcast(FP8X4),
@@ -109,7 +127,7 @@ def tile_list_tabw_none_kernel(tc, tab, w, offs, out):
             )
 
         def multiply(c):
-            a, first, last, share = CHUNKS[c]
+            a, first, last, share, load = CHUNKS[c]
             for m in range(first // M_TILE, last // M_TILE):
                 cols = slice(m * M_TILE - first, (m + 1) * M_TILE - first)
                 for begin, end, copy, queue in PARTS[m]:
@@ -130,7 +148,7 @@ def tile_list_tabw_none_kernel(tc, tab, w, offs, out):
             if RESULT_ON[m] is None:
                 result = held.tile([M_TILE, S], F32, name=f"result{m}")[:]
             else:
-                result = raws[RESULT_ON[m]][:].rearrange("p j c -> p (j c)")[:, 0:S]
+                result = raws[RESULT_ON[m][0]][:].rearrange("p j c -> p (j c)")[:, RESULT_ON[m][1] * S : (RESULT_ON[m][1] + 1) * S]
             done = 0
             for begin, end, copy, queue in PARTS[m]:
                 if copy == "vector":
@@ -151,31 +169,33 @@ def tile_list_tabw_none_kernel(tc, tab, w, offs, out):
         load_scales(1, nc.sync)
         load_scales(2, nc.sync)
         load_scales(3, nc.sync)
-        load_chunk(0)
+        load_pair(0)
+        load_pair(1)
         load_chunk(1)
         load_chunk(2)
         load_chunk(3)
-        load_chunk(4)
-        load_chunk(5)
         pick(0)
         pick(1)
         pick_scales()
-        weave(0)
+        weave_pair(nc.scalar.copy, 1, 0, 0, 256)
+        weave_pair(nc.scalar.copy, 0, 0, 192, 256)
+        weave_pair(nc.vector.tensor_copy, 0, 0, 0, 192)
+        weave_pair(nc.vector.tensor_copy, 0, 1, 0, 256)
+        weave_pair(nc.scalar.copy, 1, 1, 0, 256)
         quantize(0)
         multiply(0)
-        weave(1)
-        weave(2)
         quantize(1)
         multiply(1)
+        weave(2)
+        weave(3)
         quantize(2)
         multiply(2)
-        weave(3)
         quantize(3)
         multiply(3)
-        store(0)
         weave(4)
         quantize(4)
         multiply(4)
+        store(0)
         weave(5)
         quantize(5)
         multiply(5)

@@ -17,30 +17,12 @@ P = 128
 PACK = 4
 PASSES = K // (P * PACK)
 M_TILE = 128
-CHUNKS = (
-    (0, 0, 256, 0, 0),
-    (0, 256, 512, 0, 0),
-    (1, 0, 128, 128, 1),
-    (1, 128, 256, 0, 1),
-    (1, 256, 384, 64, 2),
-    (1, 384, 512, 80, 3),
-)
-PLACES = ((0, True), (256, True), (256, True), (512, True), (320, True), (None, True))
-RESULT_ON = (None, None, None, None)
-LOADS = ((0, 0, 512), (1, 0, 256), (1, 256, 384), (1, 384, 512))
-LAST_ON = 2
-PARTS = (((0, S, "scalar", "sync"),), ((0, S, "vector", "sync"),), ((0, S, "scalar", "sync"),), ((0, 128, "vector", "none"), (128, S, "scalar", "sync")))
-
-
-def interleave(copy, grouped, raw, first, last):
-    copy(
-        out=grouped[:, first:last, :].rearrange("p (c i) t -> p c t i", i=4),
-        in_=raw[:, :, first:last].rearrange("p t (c i) -> p c t i", i=4),
-    )
+PARTS = (((0, S, "scalar", "sync"),), ((0, S, "scalar", "sync"),), ((0, 128, "vector", "none"), (128, S, "scalar", "sync")), ((0, 128, "vector", "none"), (128, S, "scalar", "sync")))
 
 
 def tile_list_tabw_none_kernel(tc, tab, w, offs, out):
     nc = tc.nc
+    vector, scalar = nc.vector.tensor_copy, nc.scalar.copy
     with ExitStack() as ctx:
         held = ctx.enter_context(tc.tile_pool(name="held", bufs=1))
         psum = ctx.enter_context(tc.psum_pool(name="psum", bufs=1))
@@ -50,16 +32,10 @@ def tile_list_tabw_none_kernel(tc, tab, w, offs, out):
         row = T // 4
         w_rows = w.rearrange("(a p j) m -> a p j m", p=P, j=PACK)
         words = {}
-        raws = {}
         picked = {}
-        codes = {}
-        planes = {}
-        grouped = {}
         sums = {}
         tab_scales = held.tile([P, T // 4], I32, name="tab_scales", align_bytes=64)
         picked_scales = held.tile([P, S], U8, name="picked_scales", align_bytes=64)
-
-        ring = held.tile([P, 640, PACK], BF16, name="ring", align_bytes=64)
 
         def load_words(a):
             words[a] = held.tile([P, T], I32, name=f"words{a}", align_bytes=64)[:]
@@ -71,26 +47,15 @@ def tile_list_tabw_none_kernel(tc, tab, w, offs, out):
             for a in range(PASSES):
                 words[a] = both[:, a, :]
 
-        def load_scales(q, queue):
-            rows = tab_words[:, P * T + 4 * q * row : P * T + 4 * (q + 1) * row]
-            queue.dma_start(tab_scales[32 * q : 32 * q + 8, :], rows.rearrange("a (r t) -> a r t", r=4))
+        def load_scales(queue):
+            for q in range(4):
+                rows = tab_words[:, P * T + 4 * q * row : P * T + 4 * (q + 1) * row]
+                queue.dma_start(tab_scales[32 * q : 32 * q + 8, :], rows.rearrange("a (r t) -> a r t", r=4))
 
-        def load_chunk(c):
-            a, first, last = LOADS[c]
-            raws[c] = held.tile([P, PACK, last - first], F32, name=f"raw{c}", align_bytes=64)
-            nc.sync.dma_start(raws[c][:], w_rows[a][:, :, first:last])
-
-        def load_pair(u):
-            if u == 0:
-                raws[0] = held.tile([P, PACK, M], F32, name="raw0", align_bytes=64)
-            nc.sync.dma_start(raws[0][:, 2 * u : 2 * u + 2, :], w_rows[0][:, 2 * u : 2 * u + 2, :])
-
-        def weave_pair(copy, c, u, begin, end):
-            a, first, last, share, load = CHUNKS[c]
-            start, vector_first = PLACES[c]
-            grouped[c] = ring[:, start : start + last - first, :]
-            rows = slice(2 * u, 2 * u + 2)
-            interleave(copy, grouped[c][:, :, rows], raws[0][:, rows, first:last], begin, end)
+        def load(name, a, j0, j1, first, last):
+            raw = held.tile([P, j1 - j0, last - first], F32, name=name, tag=name, align_bytes=64)
+            nc.sync.dma_start(raw[:], w_rows[a][:, j0:j1, first:last])
+            return (raw, j0, j1, first)
 
         def pick(a):
             picked[a] = held.tile([P, S], U32, name=f"picked{a}", align_bytes=64)
@@ -99,35 +64,26 @@ def tile_list_tabw_none_kernel(tc, tab, w, offs, out):
         def pick_scales():
             nc.vector.tensor_copy(picked_scales[:], tab_scales[:].bitcast(U8).indirect(offsets[:]))
 
-        def weave(c):
-            a, first, last, share, load = CHUNKS[c]
-            width = last - first
-            raw = raws[load][:, :, first - LOADS[load][1] : last - LOADS[load][1]]
-            start, vector_first = PLACES[c]
-            if start is None:
-                grouped[c] = held.tile([P, width, PACK], BF16, name=f"grouped{c}", tag=f"codes{LAST_ON}", align_bytes=64)[:]
-            else:
-                grouped[c] = ring[:, start : start + width, :]
-            cut = share if vector_first else width - share
-            engines = (nc.vector.tensor_copy, nc.scalar.copy) if vector_first else (nc.scalar.copy, nc.vector.tensor_copy)
-            if cut > 0:
-                interleave(engines[0], grouped[c], raw, 0, cut)
-            if cut < width:
-                interleave(engines[1], grouped[c], raw, cut, width)
+        def group(name, first, last, tag):
+            return (held.tile([P, last - first, PACK], BF16, name=name, tag=tag, align_bytes=64), first)
 
-        def quantize(c):
-            a, first, last, share, load = CHUNKS[c]
-            width = last - first
-            codes[c] = held.tile([P, width], U32, name=f"codes{c}", tag=f"codes{c}", align_bytes=64)
-            planes[c] = held.tile([P, width], U8, name=f"plane{c}", align_bytes=64)
-            nc.vector.quantize_mx(
-                out=codes[c][:].bitcast(FP8X4),
-                scales=planes[c][:],
-                in_=grouped[c].rearrange("p w j -> p (w j)"),
+        def weave(copy, grouped, loaded, first, last):
+            tile, base = grouped
+            raw, j0, j1, raw_base = loaded
+            copy(
+                out=tile[:, first - base : last - base, j0:j1].rearrange("p (c i) t -> p c t i", i=4),
+                in_=raw[:, :, first - raw_base : last - raw_base].rearrange("p t (c i) -> p c t i", i=4),
             )
 
-        def multiply(c):
-            a, first, last, share, load = CHUNKS[c]
+        def quantize(a, grouped, first, last):
+            tile, base = grouped
+            codes = held.tile([P, last - first], U32, name=f"codes{a}_{first}", tag=f"codes{a}_{first}", align_bytes=64)
+            plane = held.tile([P, last - first], U8, name=f"plane{a}_{first}", align_bytes=64)
+            nc.vector.quantize_mx(
+                out=codes[:].bitcast(FP8X4),
+                scales=plane[:],
+                in_=tile[:, first - base : last - base, :].rearrange("p w j -> p (w j)"),
+            )
             for m in range(first // M_TILE, last // M_TILE):
                 cols = slice(m * M_TILE - first, (m + 1) * M_TILE - first)
                 for begin, end, copy, queue in PARTS[m]:
@@ -136,19 +92,16 @@ def tile_list_tabw_none_kernel(tc, tab, w, offs, out):
                         sums[m, begin] = psum.tile([M_TILE, end - begin], F32, name=f"sum{m}_{begin}")
                     nc.tensor.matmul_mx(
                         out=sums[m, begin][:],
-                        lhsT=codes[c][:, cols].bitcast(FP8X4),
-                        lhsT_scale=planes[c][:, cols],
+                        lhsT=codes[:, cols].bitcast(FP8X4),
+                        lhsT_scale=plane[:, cols],
                         rhs=picked[a][:, begin:end].bitcast(FP8X4),
                         rhs_scale=picked_scales[4 * a :, begin:end],
                         start=opens,
                         stop=not opens,
                     )
 
-        def store(m):
-            if RESULT_ON[m] is None:
-                result = held.tile([M_TILE, S], F32, name=f"result{m}")[:]
-            else:
-                result = raws[RESULT_ON[m][0]][:].rearrange("p j c -> p (j c)")[:, RESULT_ON[m][1] * S : (RESULT_ON[m][1] + 1) * S]
+        def store(m, tag):
+            result = held.tile([M_TILE, S], F32, name=f"result{m}", tag=tag, align_bytes=64)
             done = 0
             for begin, end, copy, queue in PARTS[m]:
                 if copy == "vector":
@@ -163,42 +116,42 @@ def tile_list_tabw_none_kernel(tc, tab, w, offs, out):
                     done = end
 
         nc.vector.memset(tab_scales[:], 0)
-        load_both_words()
+        r0a = load("r0a", 0, 0, 2, 0, 512)
         nc.sync.dma_start(offsets[:], offs)
-        load_scales(0, nc.sync)
-        load_scales(1, nc.sync)
-        load_scales(2, nc.sync)
-        load_scales(3, nc.sync)
-        load_pair(0)
-        load_pair(1)
-        load_chunk(1)
-        load_chunk(2)
-        load_chunk(3)
+        load_scales(nc.sync)
+        load_both_words()
+        r0b = load("r0b", 0, 2, 4, 0, 512)
+        r1a = load("r1a", 1, 0, 4, 0, 256)
+        r1b = load("r1b", 1, 0, 2, 256, 512)
+        r1c = load("r1c", 1, 2, 4, 256, 384)
+        r1d = load("r1d", 1, 2, 4, 384, 512)
+        g0 = group("g0", 0, 512, "g0")
+        weave(vector, g0, r0a, 0, 320)
+        weave(scalar, g0, r0a, 320, 512)
+        pick_scales()
         pick(0)
         pick(1)
-        pick_scales()
-        weave_pair(nc.scalar.copy, 1, 0, 0, 256)
-        weave_pair(nc.scalar.copy, 0, 0, 192, 256)
-        weave_pair(nc.vector.tensor_copy, 0, 0, 0, 192)
-        weave_pair(nc.vector.tensor_copy, 0, 1, 0, 256)
-        weave_pair(nc.scalar.copy, 1, 1, 0, 256)
-        quantize(0)
-        multiply(0)
-        quantize(1)
-        multiply(1)
-        weave(2)
-        weave(3)
-        quantize(2)
-        multiply(2)
-        quantize(3)
-        multiply(3)
-        weave(4)
-        quantize(4)
-        multiply(4)
-        store(0)
-        weave(5)
-        quantize(5)
-        multiply(5)
-        store(1)
-        store(2)
-        store(3)
+        weave(vector, g0, r0b, 0, 128)
+        weave(vector, g0, r0b, 128, 256)
+        weave(scalar, g0, r0b, 256, 512)
+        quantize(0, g0, 0, 128)
+        quantize(0, g0, 128, 256)
+        quantize(0, g0, 256, 512)
+        g10 = group("g10", 0, 128, "g10")
+        g11 = group("g11", 128, 256, "g11")
+        g12 = group("g12", 256, 384, "g12")
+        weave(vector, g10, r1a, 0, 128)
+        weave(scalar, g11, r1a, 128, 256)
+        quantize(1, g10, 0, 128)
+        quantize(1, g11, 128, 256)
+        g13 = group("g13", 384, 512, "g11")
+        weave(scalar, g12, r1b, 256, 384)
+        weave(vector, g13, r1b, 384, 512)
+        weave(scalar, g12, r1c, 256, 384)
+        weave(vector, g13, r1d, 384, 512)
+        quantize(1, g12, 256, 384)
+        quantize(1, g13, 384, 512)
+        store(0, "r1c")
+        store(1, "result1")
+        store(2, "result2")
+        store(3, "result3")

@@ -100,8 +100,11 @@ def tile_list_tabw_none_kernel(tc, tab, w, offs, out):
                         stop=not opens,
                     )
 
-        def store(m, tag):
-            result = held.tile([M_TILE, S], F32, name=f"result{m}", tag=tag, align_bytes=64)
+        def store(m, tag, on=None, half=0):
+            if on is None:
+                result = held.tile([M_TILE, S], F32, name=f"result{m}", tag=tag, align_bytes=64)[:]
+            else:
+                result = on[0][:].rearrange("p j c -> p (j c)")[:, half * S : (half + 1) * S]
             done = 0
             for begin, end, copy, queue in PARTS[m]:
                 if copy == "vector":
@@ -116,42 +119,41 @@ def tile_list_tabw_none_kernel(tc, tab, w, offs, out):
                     done = end
 
         nc.vector.memset(tab_scales[:], 0)
-        r0a = load("r0a", 0, 0, 2, 0, 512)
         nc.sync.dma_start(offsets[:], offs)
+        r0a = load("r0a", 0, 0, 2, 0, 512)
         load_scales(nc.sync)
-        load_both_words()
         r0b = load("r0b", 0, 2, 4, 0, 512)
+        load_words(0)
         r1a = load("r1a", 1, 0, 4, 0, 256)
-        r1b = load("r1b", 1, 0, 2, 256, 512)
-        r1c = load("r1c", 1, 2, 4, 256, 384)
-        r1d = load("r1d", 1, 2, 4, 384, 512)
-        g0 = group("g0", 0, 512, "g0")
-        weave(vector, g0, r0a, 0, 320)
-        weave(scalar, g0, r0a, 320, 512)
+        load_words(1)
+        r1c = load("r1c", 1, 0, 4, 256, 384)
+        r1d = load("r1d", 1, 0, 4, 384, 512)
+        g0a = group("g0a", 0, 256, "g0a")
+        g0b = group("g0b", 256, 512, "g0b")
+        weave(vector, g0a, r0a, 0, 256)
+        weave(scalar, g0b, r0a, 256, 512)
         pick_scales()
+        weave(vector, g0a, r0b, 0, 256)
+        weave(scalar, g0b, r0b, 256, 512)
         pick(0)
-        pick(1)
-        weave(vector, g0, r0b, 0, 128)
-        weave(vector, g0, r0b, 128, 256)
-        weave(scalar, g0, r0b, 256, 512)
-        quantize(0, g0, 0, 128)
-        quantize(0, g0, 128, 256)
-        quantize(0, g0, 256, 512)
+        quantize(0, g0a, 0, 256)
+        quantize(0, g0b, 256, 512)
         g10 = group("g10", 0, 128, "g10")
         g11 = group("g11", 128, 256, "g11")
         g12 = group("g12", 256, 384, "g12")
-        weave(vector, g10, r1a, 0, 128)
-        weave(scalar, g11, r1a, 128, 256)
+        weave(scalar, g10, r1a, 0, 128)
+        weave(scalar, g11, r1a, 128, 192)
+        weave(vector, g11, r1a, 192, 256)
+        pick(1)
         quantize(1, g10, 0, 128)
         quantize(1, g11, 128, 256)
-        g13 = group("g13", 384, 512, "g11")
-        weave(scalar, g12, r1b, 256, 384)
-        weave(vector, g13, r1b, 384, 512)
         weave(scalar, g12, r1c, 256, 384)
-        weave(vector, g13, r1d, 384, 512)
+        g13 = group("g13", 384, 512, "g11")
+        weave(vector, g13, r1d, 384, 480)
+        weave(scalar, g13, r1d, 480, 512)
         quantize(1, g12, 256, 384)
         quantize(1, g13, 384, 512)
-        store(0, "r1c")
-        store(1, "result1")
-        store(2, "result2")
+        store(0, "", r1c, 0)
+        store(1, "", r1d, 1)
+        store(2, "g11")
         store(3, "result3")

@@ -15,80 +15,77 @@ FP8X4 = mybir.dt.float8_e4m3fn_x4
 
 P = 128
 PACK = 4
-PASSES = K // (P * PACK)
+PAIR = 2
+QUADRANT = 32
 M_TILE = 128
-PARTS = (((0, S, "scalar", "sync"),), ((0, S, "scalar", "sync"),), ((0, 128, "vector", "none"), (128, S, "scalar", "sync")), ((0, 128, "vector", "none"), (128, S, "scalar", "sync")))
+M_HALF = M // 2
+S_HALF = S // 2
+VECTOR_OF_TILE_1 = 64
+VECTOR_OF_TILE_3 = 96
 
 
 def tile_list_tabw_none_kernel(tc, tab, w, offs, out):
     nc = tc.nc
-    vector, scalar = nc.vector.tensor_copy, nc.scalar.copy
+    vector_copy, scalar_copy = nc.vector.tensor_copy, nc.scalar.copy
+    by_scalar = ((0, S_HALF, scalar_copy), (S_HALF, S, scalar_copy))
+    by_both = ((0, S_HALF, vector_copy), (S_HALF, S, scalar_copy))
+    parts = (by_scalar, by_scalar, by_both, by_both)
     with ExitStack() as ctx:
         held = ctx.enter_context(tc.tile_pool(name="held", bufs=1))
         psum = ctx.enter_context(tc.psum_pool(name="psum", bufs=1))
 
         offsets = held.tile([P, S // 16], U16, name="offsets")
         tab_words = tab.bitcast(I32)
-        row = T // 4
-        w_rows = w.rearrange("(a p j) m -> a p j m", p=P, j=PACK)
-        words = {}
+        scale_row = T // 4
+        w_rows = w.rearrange("(a p t) n -> a p t n", p=P, t=PACK)
         picked = {}
         sums = {}
-        tab_scales = held.tile([P, T // 4], I32, name="tab_scales", align_bytes=64)
+        tab_scales = held.tile([P, scale_row], I32, name="tab_scales", align_bytes=64)
         picked_scales = held.tile([P, S], U8, name="picked_scales", align_bytes=64)
 
         def load_words(a):
-            words[a] = held.tile([P, T], I32, name=f"words{a}", align_bytes=64)[:]
-            nc.sync.dma_start(words[a], tab_words[a, 0 : P * T].rearrange("(p t) -> p t", p=P))
+            words = held.tile([P, T], I32, name=f"words{a}", align_bytes=64)
+            nc.sync.dma_start(words[:], tab_words[a, 0 : P * T].rearrange("(p c) -> p c", p=P))
+            return words
 
-        def load_both_words():
-            both = held.tile([P, PASSES, T], I32, name="words", align_bytes=64)
-            nc.sync.dma_start(both[:], tab_words[:, 0 : P * T].rearrange("a (p t) -> p a t", p=P))
-            for a in range(PASSES):
-                words[a] = both[:, a, :]
+        def load_scales():
+            for quad in range(P // QUADRANT):
+                rows = tab_words[:, P * T + 4 * quad * scale_row : P * T + 4 * (quad + 1) * scale_row]
+                nc.sync.dma_start(tab_scales[QUADRANT * quad : QUADRANT * quad + 8, :], rows.rearrange("a (r c) -> a r c", r=4))
 
-        def load_scales(queue):
-            for q in range(4):
-                rows = tab_words[:, P * T + 4 * q * row : P * T + 4 * (q + 1) * row]
-                queue.dma_start(tab_scales[32 * q : 32 * q + 8, :], rows.rearrange("a (r t) -> a r t", r=4))
+        def load_w(name, a, t0, t1, first, last):
+            raw = held.tile([P, t1 - t0, last - first], F32, name=name, tag=name, align_bytes=64)
+            nc.sync.dma_start(raw[:], w_rows[a][:, t0:t1, first:last])
+            return (raw, t0, t1, first)
 
-        def load(name, a, j0, j1, first, last):
-            raw = held.tile([P, j1 - j0, last - first], F32, name=name, tag=name, align_bytes=64)
-            nc.sync.dma_start(raw[:], w_rows[a][:, j0:j1, first:last])
-            return (raw, j0, j1, first)
-
-        def pick(a):
+        def pick_words(a, words):
             picked[a] = held.tile([P, S], U32, name=f"picked{a}", align_bytes=64)
-            nc.vector.tensor_copy(picked[a][:], words[a].bitcast(U32).indirect(offsets[:]))
+            nc.vector.tensor_copy(picked[a][:], words[:].bitcast(U32).indirect(offsets[:]))
 
-        def pick_scales():
-            nc.vector.tensor_copy(picked_scales[:], tab_scales[:].bitcast(U8).indirect(offsets[:]))
-
-        def group(name, first, last, tag):
+        def interleaved(name, first, last, tag):
             return (held.tile([P, last - first, PACK], BF16, name=name, tag=tag, align_bytes=64), first)
 
         def weave(copy, grouped, loaded, first, last):
-            tile, base = grouped
-            raw, j0, j1, raw_base = loaded
+            tile, tile_first = grouped
+            raw, t0, t1, raw_first = loaded
             copy(
-                out=tile[:, first - base : last - base, j0:j1].rearrange("p (c i) t -> p c t i", i=4),
-                in_=raw[:, :, first - raw_base : last - raw_base].rearrange("p t (c i) -> p c t i", i=4),
+                out=tile[:, first - tile_first : last - tile_first, t0:t1].rearrange("p (c i) t -> p c t i", i=4),
+                in_=raw[:, :, first - raw_first : last - raw_first].rearrange("p t (c i) -> p c t i", i=4),
             )
 
-        def quantize(a, grouped, first, last):
-            tile, base = grouped
+        def quantize_and_multiply(a, grouped, first, last):
+            tile, tile_first = grouped
             codes = held.tile([P, last - first], U32, name=f"codes{a}_{first}", tag=f"codes{a}_{first}", align_bytes=64)
             plane = held.tile([P, last - first], U8, name=f"plane{a}_{first}", align_bytes=64)
             nc.vector.quantize_mx(
                 out=codes[:].bitcast(FP8X4),
                 scales=plane[:],
-                in_=tile[:, first - base : last - base, :].rearrange("p w j -> p (w j)"),
+                in_=tile[:, first - tile_first : last - tile_first, :].rearrange("p c t -> p (c t)"),
             )
             for m in range(first // M_TILE, last // M_TILE):
                 cols = slice(m * M_TILE - first, (m + 1) * M_TILE - first)
-                for begin, end, copy, queue in PARTS[m]:
-                    opens = (m, begin) not in sums
-                    if opens:
+                for begin, end, copy in parts[m]:
+                    if a == 0:
                         sums[m, begin] = psum.tile([M_TILE, end - begin], F32, name=f"sum{m}_{begin}")
                     nc.tensor.matmul_mx(
                         out=sums[m, begin][:],
@@ -96,64 +93,58 @@ def tile_list_tabw_none_kernel(tc, tab, w, offs, out):
                         lhsT_scale=plane[:, cols],
                         rhs=picked[a][:, begin:end].bitcast(FP8X4),
                         rhs_scale=picked_scales[4 * a :, begin:end],
-                        start=opens,
-                        stop=not opens,
+                        start=(a == 0),
+                        stop=(a == 1),
                     )
 
-        def store(m, tag, on=None, half=0):
-            if on is None:
-                result = held.tile([M_TILE, S], F32, name=f"result{m}", tag=tag, align_bytes=64)[:]
-            else:
-                result = on[0][:].rearrange("p j c -> p (j c)")[:, half * S : (half + 1) * S]
-            done = 0
-            for begin, end, copy, queue in PARTS[m]:
-                if copy == "vector":
-                    nc.vector.tensor_copy(out=result[:, begin:end], in_=sums[m, begin][:])
-                else:
-                    nc.scalar.copy(out=result[:, begin:end], in_=sums[m, begin][:])
-                if queue == "sync":
-                    nc.sync.dma_start(out=out[m * M_TILE : (m + 1) * M_TILE, done:end], in_=result[:, done:end])
-                    done = end
-                if queue == "scalar":
-                    nc.scalar.dma_start(out=out[m * M_TILE : (m + 1) * M_TILE, done:end], in_=result[:, done:end])
-                    done = end
+        def store(m, result):
+            for begin, end, copy in parts[m]:
+                copy(out=result[:, begin:end], in_=sums[m, begin][:])
+            nc.sync.dma_start(out=out[m * M_TILE : (m + 1) * M_TILE, 0:S], in_=result[:, 0:S])
+
+        def staged_on(loaded, place):
+            return loaded[0][:].rearrange("p t c -> p (t c)")[:, place * S : (place + 1) * S]
 
         nc.vector.memset(tab_scales[:], 0)
+
+        w0_low = load_w("r0a", 0, 0, PAIR, 0, M)
         nc.sync.dma_start(offsets[:], offs)
-        r0a = load("r0a", 0, 0, 2, 0, 512)
-        load_scales(nc.sync)
-        r0b = load("r0b", 0, 2, 4, 0, 512)
-        load_words(0)
-        r1a = load("r1a", 1, 0, 4, 0, 256)
-        load_words(1)
-        r1c = load("r1c", 1, 0, 4, 256, 384)
-        r1d = load("r1d", 1, 0, 4, 384, 512)
-        g0a = group("g0a", 0, 256, "g0a")
-        g0b = group("g0b", 256, 512, "g0b")
-        weave(vector, g0a, r0a, 0, 256)
-        weave(scalar, g0b, r0a, 256, 512)
-        pick_scales()
-        weave(vector, g0a, r0b, 0, 256)
-        weave(scalar, g0b, r0b, 256, 512)
-        pick(0)
-        quantize(0, g0a, 0, 256)
-        quantize(0, g0b, 256, 512)
-        g10 = group("g10", 0, 128, "g10")
-        g11 = group("g11", 128, 256, "g11")
-        g12 = group("g12", 256, 384, "g12")
-        weave(scalar, g10, r1a, 0, 128)
-        weave(scalar, g11, r1a, 128, 192)
-        weave(vector, g11, r1a, 192, 256)
-        pick(1)
-        quantize(1, g10, 0, 128)
-        quantize(1, g11, 128, 256)
-        weave(scalar, g12, r1c, 256, 384)
-        g13 = group("g13", 384, 512, "g11")
-        weave(vector, g13, r1d, 384, 480)
-        weave(scalar, g13, r1d, 480, 512)
-        quantize(1, g12, 256, 384)
-        quantize(1, g13, 384, 512)
-        store(0, "", r1c, 0)
-        store(1, "", r1d, 1)
-        store(2, "g11")
-        store(3, "result3")
+        load_scales()
+        words0 = load_words(0)
+        w0_high = load_w("r0b", 0, PAIR, PACK, 0, M)
+        w1_left = load_w("r1a", 1, 0, PACK, 0, M_HALF)
+        words1 = load_words(1)
+        w1_tile2 = load_w("r1c", 1, 0, PACK, 2 * M_TILE, 3 * M_TILE)
+        w1_tile3 = load_w("r1d", 1, 0, PACK, 3 * M_TILE, M)
+
+        left = interleaved("g0a", 0, M_HALF, "g0a")
+        right = interleaved("g0b", M_HALF, M, "g0b")
+        weave(vector_copy, left, w0_low, 0, M_HALF)
+        weave(scalar_copy, right, w0_low, M_HALF, M)
+        nc.vector.tensor_copy(picked_scales[:], tab_scales[:].bitcast(U8).indirect(offsets[:]))
+        pick_words(0, words0)
+        weave(vector_copy, left, w0_high, 0, M_HALF)
+        weave(scalar_copy, right, w0_high, M_HALF, M)
+        quantize_and_multiply(0, left, 0, M_HALF)
+        quantize_and_multiply(0, right, M_HALF, M)
+
+        tile0 = interleaved("g10", 0, M_TILE, "g10")
+        tile1 = interleaved("g11", M_TILE, 2 * M_TILE, "g11")
+        tile2 = interleaved("g12", 2 * M_TILE, 3 * M_TILE, "g12")
+        weave(scalar_copy, tile0, w1_left, 0, M_TILE)
+        weave(scalar_copy, tile1, w1_left, M_TILE, 2 * M_TILE - VECTOR_OF_TILE_1)
+        weave(vector_copy, tile1, w1_left, 2 * M_TILE - VECTOR_OF_TILE_1, 2 * M_TILE)
+        pick_words(1, words1)
+        quantize_and_multiply(1, tile0, 0, M_TILE)
+        quantize_and_multiply(1, tile1, M_TILE, 2 * M_TILE)
+        weave(scalar_copy, tile2, w1_tile2, 2 * M_TILE, 3 * M_TILE)
+        tile3 = interleaved("g13", 3 * M_TILE, M, "g11")
+        weave(vector_copy, tile3, w1_tile3, 3 * M_TILE, 3 * M_TILE + VECTOR_OF_TILE_3)
+        weave(scalar_copy, tile3, w1_tile3, 3 * M_TILE + VECTOR_OF_TILE_3, M)
+        quantize_and_multiply(1, tile2, 2 * M_TILE, 3 * M_TILE)
+        quantize_and_multiply(1, tile3, 3 * M_TILE, M)
+
+        store(0, staged_on(w1_tile2, 0))
+        store(1, staged_on(w1_tile3, 1))
+        store(2, held.tile([M_TILE, S], F32, name="result2", tag="g11", align_bytes=64)[:])
+        store(3, held.tile([M_TILE, S], F32, name="result3", tag="result3", align_bytes=64)[:])

@@ -20,8 +20,6 @@ QUADRANT = 32
 M_TILE = 128
 M_HALF = M // 2
 S_HALF = S // 2
-VECTOR_OF_TILE_1 = 64
-VECTOR_OF_TILE_3 = 96
 
 
 def tile_list_tabw_none_kernel(tc, tab, w, offs, out):
@@ -39,49 +37,38 @@ def tile_list_tabw_none_kernel(tc, tab, w, offs, out):
         scale_row = T // 4
         w_rows = w.rearrange("(a p t) n -> a p t n", p=P, t=PACK)
         picked = {}
+        picked_scales = {}
         sums = {}
-        tab_scales = held.tile([P, scale_row], I32, name="tab_scales", align_bytes=64)
-        picked_scales = held.tile([P, S], U8, name="picked_scales", align_bytes=64)
-
-        def load_words(a):
-            words = held.tile([P, T], I32, name=f"words{a}", align_bytes=64)
-            nc.sync.dma_start(words[:], tab_words[a, 0 : P * T].rearrange("(p c) -> p c", p=P))
-            return words
+        tab_scales = held.tile([P, 2, scale_row], I32, name="tab_scales", align_bytes=64)
+        words = held.tile([P, 2, T], I32, name="words", align_bytes=64)
+        raw0 = held.tile([P, PACK, M], F32, name="raw0", align_bytes=64)
+        raw1 = held.tile([P, PACK, M], F32, name="raw1", align_bytes=64)
 
         def load_scales():
-            for quad in range(P // QUADRANT):
-                rows = tab_words[:, P * T + 4 * quad * scale_row : P * T + 4 * (quad + 1) * scale_row]
-                nc.sync.dma_start(tab_scales[QUADRANT * quad : QUADRANT * quad + 8, :], rows.rearrange("a (r c) -> a r c", r=4))
+            rows = tab_words[:, P * T :].rearrange("a (q r c) -> r q a c", r=4, c=scale_row)
+            for r in range(4):
+                nc.sync.dma_start(tab_scales[r:P:QUADRANT, :, :], rows[r])
 
-        def load_w(name, a, t0, t1, first, last):
-            raw = held.tile([P, t1 - t0, last - first], F32, name=name, tag=name, align_bytes=64)
-            nc.sync.dma_start(raw[:], w_rows[a][:, t0:t1, first:last])
-            return (raw, t0, t1, first)
-
-        def pick_words(a, words):
+        def pick_words(a):
             picked[a] = held.tile([P, S], U32, name=f"picked{a}", align_bytes=64)
-            nc.vector.tensor_copy(picked[a][:], words[:].bitcast(U32).indirect(offsets[:]))
+            nc.vector.tensor_copy(picked[a][:], words[:, a, :].bitcast(U32).indirect(offsets[:]))
 
-        def interleaved(name, first, last, tag):
-            return (held.tile([P, last - first, PACK], BF16, name=name, tag=tag, align_bytes=64), first)
+        def pick_scales(a):
+            picked_scales[a] = held.tile([P, S], U8, name=f"picked_scales{a}", align_bytes=64)
+            nc.vector.tensor_copy(picked_scales[a][:], tab_scales[:, a, :].bitcast(U8).indirect(offsets[:]))
 
-        def weave(copy, grouped, loaded, first, last):
-            tile, tile_first = grouped
-            raw, t0, t1, raw_first = loaded
+        def weave(copy, raw, name, tag, first, last):
+            tile = held.tile([P, last - first, PACK], BF16, name=name, tag=tag, align_bytes=64)
             copy(
-                out=tile[:, first - tile_first : last - tile_first, t0:t1].rearrange("p (c i) t -> p c t i", i=4),
-                in_=raw[:, :, first - raw_first : last - raw_first].rearrange("p t (c i) -> p c t i", i=4),
+                out=tile[:].rearrange("p (c i) t -> p c t i", i=4),
+                in_=raw[:, :, first:last].rearrange("p t (c i) -> p c t i", i=4),
             )
+            return tile
 
-        def quantize_and_multiply(a, grouped, first, last):
-            tile, tile_first = grouped
+        def quantize_and_multiply(a, tile, first, last):
             codes = held.tile([P, last - first], U32, name=f"codes{a}_{first}", tag=f"codes{a}_{first}", align_bytes=64)
             plane = held.tile([P, last - first], U8, name=f"plane{a}_{first}", align_bytes=64)
-            nc.vector.quantize_mx(
-                out=codes[:].bitcast(FP8X4),
-                scales=plane[:],
-                in_=tile[:, first - tile_first : last - tile_first, :].rearrange("p c t -> p (c t)"),
-            )
+            nc.vector.quantize_mx(out=codes[:].bitcast(FP8X4), scales=plane[:], in_=tile[:].rearrange("p c t -> p (c t)"))
             for m in range(first // M_TILE, last // M_TILE):
                 cols = slice(m * M_TILE - first, (m + 1) * M_TILE - first)
                 for begin, end, copy in parts[m]:
@@ -92,7 +79,7 @@ def tile_list_tabw_none_kernel(tc, tab, w, offs, out):
                         lhsT=codes[:, cols].bitcast(FP8X4),
                         lhsT_scale=plane[:, cols],
                         rhs=picked[a][:, begin:end].bitcast(FP8X4),
-                        rhs_scale=picked_scales[4 * a :, begin:end],
+                        rhs_scale=picked_scales[a][:, begin:end],
                         start=(a == 0),
                         stop=(a == 1),
                     )
@@ -102,49 +89,38 @@ def tile_list_tabw_none_kernel(tc, tab, w, offs, out):
                 copy(out=result[:, begin:end], in_=sums[m, begin][:])
             nc.sync.dma_start(out=out[m * M_TILE : (m + 1) * M_TILE, 0:S], in_=result[:, 0:S])
 
-        def staged_on(loaded, place):
-            return loaded[0][:].rearrange("p t c -> p (t c)")[:, place * S : (place + 1) * S]
-
         nc.vector.memset(tab_scales[:], 0)
 
-        w0_low = load_w("r0a", 0, 0, PAIR, 0, M)
+        nc.sync.dma_start(words[:], tab_words[:, 0 : P * T].rearrange("a (p c) -> p a c", p=P))
         nc.sync.dma_start(offsets[:], offs)
         load_scales()
-        words0 = load_words(0)
-        w0_high = load_w("r0b", 0, PAIR, PACK, 0, M)
-        w1_left = load_w("r1a", 1, 0, PACK, 0, M_HALF)
-        words1 = load_words(1)
-        w1_tile2 = load_w("r1c", 1, 0, PACK, 2 * M_TILE, 3 * M_TILE)
-        w1_tile3 = load_w("r1d", 1, 0, PACK, 3 * M_TILE, M)
+        nc.sync.dma_start(raw0[:], w_rows[0])
+        nc.sync.dma_start(raw1[:, 0:PAIR, :], w_rows[1][:, 0:PAIR, :])
+        for m in range(M // M_TILE):
+            cols = slice(m * M_TILE, (m + 1) * M_TILE)
+            nc.sync.dma_start(raw1[:, PAIR:PACK, cols], w_rows[1][:, PAIR:PACK, cols])
 
-        left = interleaved("g0a", 0, M_HALF, "g0a")
-        right = interleaved("g0b", M_HALF, M, "g0b")
-        weave(vector_copy, left, w0_low, 0, M_HALF)
-        weave(scalar_copy, right, w0_low, M_HALF, M)
-        nc.vector.tensor_copy(picked_scales[:], tab_scales[:].bitcast(U8).indirect(offsets[:]))
-        pick_words(0, words0)
-        weave(vector_copy, left, w0_high, 0, M_HALF)
-        weave(scalar_copy, right, w0_high, M_HALF, M)
-        quantize_and_multiply(0, left, 0, M_HALF)
-        quantize_and_multiply(0, right, M_HALF, M)
+        pick_words(0)
+        pick_words(1)
+        pick_scales(0)
+        pick_scales(1)
+        first = [
+            weave(copy, raw0, f"g0{m}", f"g0{m}", m * M_TILE, (m + 1) * M_TILE)
+            for m, copy in enumerate((vector_copy, vector_copy, scalar_copy, scalar_copy))
+        ]
+        for m in range(M // M_TILE):
+            quantize_and_multiply(0, first[m], m * M_TILE, (m + 1) * M_TILE)
 
-        tile0 = interleaved("g10", 0, M_TILE, "g10")
-        tile1 = interleaved("g11", M_TILE, 2 * M_TILE, "g11")
-        tile2 = interleaved("g12", 2 * M_TILE, 3 * M_TILE, "g12")
-        weave(scalar_copy, tile0, w1_left, 0, M_TILE)
-        weave(scalar_copy, tile1, w1_left, M_TILE, 2 * M_TILE - VECTOR_OF_TILE_1)
-        weave(vector_copy, tile1, w1_left, 2 * M_TILE - VECTOR_OF_TILE_1, 2 * M_TILE)
-        pick_words(1, words1)
+        tile0 = weave(scalar_copy, raw1, "g10", "g10", 0, M_TILE)
+        tile1 = weave(vector_copy, raw1, "g11", "g03", M_TILE, 2 * M_TILE)
+        tile2 = weave(scalar_copy, raw1, "g12", "g12", 2 * M_TILE, 3 * M_TILE)
         quantize_and_multiply(1, tile0, 0, M_TILE)
         quantize_and_multiply(1, tile1, M_TILE, 2 * M_TILE)
-        weave(scalar_copy, tile2, w1_tile2, 2 * M_TILE, 3 * M_TILE)
-        tile3 = interleaved("g13", 3 * M_TILE, M, "g11")
-        weave(vector_copy, tile3, w1_tile3, 3 * M_TILE, 3 * M_TILE + VECTOR_OF_TILE_3)
-        weave(scalar_copy, tile3, w1_tile3, 3 * M_TILE + VECTOR_OF_TILE_3, M)
+        tile3 = weave(vector_copy, raw1, "g13", "g10", 3 * M_TILE, M)
         quantize_and_multiply(1, tile2, 2 * M_TILE, 3 * M_TILE)
         quantize_and_multiply(1, tile3, 3 * M_TILE, M)
 
-        store(0, staged_on(w1_tile2, 0))
-        store(1, staged_on(w1_tile3, 1))
-        store(2, held.tile([M_TILE, S], F32, name="result2", tag="g11", align_bytes=64)[:])
+        store(0, held.tile([M_TILE, S], F32, name="result0", align_bytes=64)[:])
+        store(1, held.tile([M_TILE, S], F32, name="result1", align_bytes=64)[:])
+        store(2, held.tile([M_TILE, S], F32, name="result2", tag="result2", align_bytes=64)[:])
         store(3, held.tile([M_TILE, S], F32, name="result3", tag="result3", align_bytes=64)[:])

@@ -41,7 +41,7 @@ def tile_list_tabw_none_kernel(tc, tab, w, offs, out):
         sums = {}
         tab_scales = held.tile([P, 2, scale_row], I32, name="tab_scales", align_bytes=64)
         words = held.tile([P, 2, T], I32, name="words", align_bytes=64)
-        raw0 = held.tile([P, PACK, M], F32, name="raw0", align_bytes=64)
+        raw0 = held.tile([P, PACK, M], F32, name="raw0", tag="raw0", align_bytes=64)
         raw1 = held.tile([P, PACK, M], F32, name="raw1", align_bytes=64)
 
         def load_scales():
@@ -112,7 +112,7 @@ def tile_list_tabw_none_kernel(tc, tab, w, offs, out):
             quantize_and_multiply(0, first[m], m * M_TILE, (m + 1) * M_TILE)
 
         tile0 = weave(scalar_copy, raw1, "g10", "g10", 0, M_TILE)
-        tile1 = weave(vector_copy, raw1, "g11", "g03", M_TILE, 2 * M_TILE)
+        tile1 = weave(vector_copy, raw1, "g11", "raw0", M_TILE, 2 * M_TILE)
         tile2 = weave(scalar_copy, raw1, "g12", "g12", 2 * M_TILE, 3 * M_TILE)
         quantize_and_multiply(1, tile0, 0, M_TILE)
         quantize_and_multiply(1, tile1, M_TILE, 2 * M_TILE)

@@ -16,8 +16,12 @@ FP8X4 = mybir.dt.float8_e4m3fn_x4
 P = 128
 PACK = 4
 PAIR = 2
+PASSES = K // (P * PACK)
 QUADRANT = 32
+PLANE_ROWS = 4
+LINE = 4
 M_TILE = 128
+ROW_TILES = M // M_TILE
 M_HALF = M // 2
 S_HALF = S // 2
 
@@ -39,14 +43,14 @@ def tile_list_tabw_none_kernel(tc, tab, w, offs, out):
         picked = {}
         picked_scales = {}
         sums = {}
-        tab_scales = held.tile([P, 2, scale_row], I32, name="tab_scales", align_bytes=64)
-        words = held.tile([P, 2, T], I32, name="words", align_bytes=64)
+        tab_scales = held.tile([P, PASSES, scale_row], I32, name="tab_scales", align_bytes=64)
+        words = held.tile([P, PASSES, T], I32, name="words", align_bytes=64)
         raw0 = held.tile([P, PACK, M], F32, name="raw0", tag="raw0", align_bytes=64)
         raw1 = held.tile([P, PACK, M], F32, name="raw1", align_bytes=64)
 
         def load_scales():
-            rows = tab_words[:, P * T :].rearrange("a (q r c) -> r q a c", r=4, c=scale_row)
-            for r in range(4):
+            rows = tab_words[:, P * T :].rearrange("a (q r c) -> r q a c", r=PLANE_ROWS, c=scale_row)
+            for r in range(PLANE_ROWS):
                 nc.sync.dma_start(tab_scales[r:P:QUADRANT, :, :], rows[r])
 
         def pick_words(a):
@@ -57,34 +61,33 @@ def tile_list_tabw_none_kernel(tc, tab, w, offs, out):
             picked_scales[a] = held.tile([P, S], U8, name=f"picked_scales{a}", align_bytes=64)
             nc.vector.tensor_copy(picked_scales[a][:], tab_scales[:, a, :].bitcast(U8).indirect(offsets[:]))
 
-        def weave(copy, raw, name, tag, first, last):
-            tile = held.tile([P, last - first, PACK], BF16, name=name, tag=tag, align_bytes=64)
+        def interleave(copy, raw, name, tag, m):
+            grouped = held.tile([P, M_TILE, PACK], BF16, name=name, tag=tag, align_bytes=64)
             copy(
-                out=tile[:].rearrange("p (c i) t -> p c t i", i=4),
-                in_=raw[:, :, first:last].rearrange("p t (c i) -> p c t i", i=4),
+                out=grouped[:].rearrange("p (c i) t -> p c t i", i=LINE),
+                in_=raw[:, :, m * M_TILE : (m + 1) * M_TILE].rearrange("p t (c i) -> p c t i", i=LINE),
             )
-            return tile
+            return grouped
 
-        def quantize_and_multiply(a, tile, first, last):
-            codes = held.tile([P, last - first], U32, name=f"codes{a}_{first}", tag=f"codes{a}_{first}", align_bytes=64)
-            plane = held.tile([P, last - first], U8, name=f"plane{a}_{first}", align_bytes=64)
-            nc.vector.quantize_mx(out=codes[:].bitcast(FP8X4), scales=plane[:], in_=tile[:].rearrange("p c t -> p (c t)"))
-            for m in range(first // M_TILE, last // M_TILE):
-                cols = slice(m * M_TILE - first, (m + 1) * M_TILE - first)
-                for begin, end, copy in parts[m]:
-                    if a == 0:
-                        sums[m, begin] = psum.tile([M_TILE, end - begin], F32, name=f"sum{m}_{begin}")
-                    nc.tensor.matmul_mx(
-                        out=sums[m, begin][:],
-                        lhsT=codes[:, cols].bitcast(FP8X4),
-                        lhsT_scale=plane[:, cols],
-                        rhs=picked[a][:, begin:end].bitcast(FP8X4),
-                        rhs_scale=picked_scales[a][:, begin:end],
-                        start=(a == 0),
-                        stop=(a == 1),
-                    )
+        def quantize_and_multiply(a, grouped, m):
+            codes = held.tile([P, M_TILE], U32, name=f"codes{a}_{m}", align_bytes=64)
+            plane = held.tile([P, M_TILE], U8, name=f"plane{a}_{m}", align_bytes=64)
+            nc.vector.quantize_mx(out=codes[:].bitcast(FP8X4), scales=plane[:], in_=grouped[:].rearrange("p c t -> p (c t)"))
+            for begin, end, copy in parts[m]:
+                if a == 0:
+                    sums[m, begin] = psum.tile([M_TILE, end - begin], F32, name=f"sum{m}_{begin}")
+                nc.tensor.matmul_mx(
+                    out=sums[m, begin][:],
+                    lhsT=codes[:].bitcast(FP8X4),
+                    lhsT_scale=plane[:],
+                    rhs=picked[a][:, begin:end].bitcast(FP8X4),
+                    rhs_scale=picked_scales[a][:, begin:end],
+                    start=(a == 0),
+                    stop=(a == PASSES - 1),
+                )
 
-        def store(m, result):
+        def store(m):
+            result = held.tile([M_TILE, S], F32, name=f"result{m}", align_bytes=64)
             for begin, end, copy in parts[m]:
                 copy(out=result[:, begin:end], in_=sums[m, begin][:])
             nc.sync.dma_start(out=out[m * M_TILE : (m + 1) * M_TILE, 0:S], in_=result[:, 0:S])
@@ -95,32 +98,31 @@ def tile_list_tabw_none_kernel(tc, tab, w, offs, out):
         nc.sync.dma_start(offsets[:], offs)
         load_scales()
         nc.sync.dma_start(raw0[:], w_rows[0])
-        nc.sync.dma_start(raw1[:, 0:PAIR, :], w_rows[1][:, 0:PAIR, :])
-        for m in range(M // M_TILE):
+        nc.sync.dma_start(raw1[:, :, 0:M_HALF], w_rows[1][:, :, 0:M_HALF])
+        nc.sync.dma_start(raw1[:, 0:PAIR, M_HALF:M], w_rows[1][:, 0:PAIR, M_HALF:M])
+        for m in range(M_HALF // M_TILE, ROW_TILES):
             cols = slice(m * M_TILE, (m + 1) * M_TILE)
             nc.sync.dma_start(raw1[:, PAIR:PACK, cols], w_rows[1][:, PAIR:PACK, cols])
 
-        pick_words(0)
-        pick_words(1)
-        pick_scales(0)
-        pick_scales(1)
-        first = [
-            weave(copy, raw0, f"g0{m}", f"g0{m}", m * M_TILE, (m + 1) * M_TILE)
-            for m, copy in enumerate((vector_copy, vector_copy, scalar_copy, scalar_copy))
+        for a in range(PASSES):
+            pick_words(a)
+        for a in range(PASSES):
+            pick_scales(a)
+
+        grouped0 = [
+            interleave(copy, raw0, f"g0{m}", f"g0{m}", m) for m, copy in enumerate((vector_copy, vector_copy, scalar_copy, scalar_copy))
         ]
-        for m in range(M // M_TILE):
-            quantize_and_multiply(0, first[m], m * M_TILE, (m + 1) * M_TILE)
+        for m in range(ROW_TILES):
+            quantize_and_multiply(0, grouped0[m], m)
 
-        tile0 = weave(scalar_copy, raw1, "g10", "g10", 0, M_TILE)
-        tile1 = weave(vector_copy, raw1, "g11", "raw0", M_TILE, 2 * M_TILE)
-        tile2 = weave(scalar_copy, raw1, "g12", "g12", 2 * M_TILE, 3 * M_TILE)
-        quantize_and_multiply(1, tile0, 0, M_TILE)
-        quantize_and_multiply(1, tile1, M_TILE, 2 * M_TILE)
-        tile3 = weave(vector_copy, raw1, "g13", "g10", 3 * M_TILE, M)
-        quantize_and_multiply(1, tile2, 2 * M_TILE, 3 * M_TILE)
-        quantize_and_multiply(1, tile3, 3 * M_TILE, M)
+        tile0 = interleave(scalar_copy, raw1, "g10", "g10", 0)
+        tile1 = interleave(vector_copy, raw1, "g11", "raw0", 1)
+        tile2 = interleave(scalar_copy, raw1, "g12", "g12", 2)
+        quantize_and_multiply(1, tile0, 0)
+        quantize_and_multiply(1, tile1, 1)
+        tile3 = interleave(vector_copy, raw1, "g13", "g10", 3)
+        quantize_and_multiply(1, tile2, 2)
+        quantize_and_multiply(1, tile3, 3)
 
-        store(0, held.tile([M_TILE, S], F32, name="result0", align_bytes=64)[:])
-        store(1, held.tile([M_TILE, S], F32, name="result1", align_bytes=64)[:])
-        store(2, held.tile([M_TILE, S], F32, name="result2", tag="result2", align_bytes=64)[:])
-        store(3, held.tile([M_TILE, S], F32, name="result3", tag="result3", align_bytes=64)[:])
+        for m in range(ROW_TILES):
+            store(m)

@@ -96,8 +96,11 @@ def tile_list_tabw_none_kernel(tc, tab, w, offs, out):
 
         nc.sync.dma_start(words[:], tab_words[:, 0 : P * T].rearrange("a (p c) -> p a c", p=P))
         nc.sync.dma_start(offsets[:], offs)
+        raw0_run = raw0[:].rearrange("p t n -> p (t n)")
+        w0_run = w_rows[0].rearrange("p t n -> p (t n)")
+        nc.sync.dma_start(raw0_run[:, 0:M_HALF], w0_run[:, 0:M_HALF])
         load_scales()
-        nc.sync.dma_start(raw0[:], w_rows[0])
+        nc.sync.dma_start(raw0_run[:, M_HALF:], w0_run[:, M_HALF:])
         nc.sync.dma_start(raw1[:, :, 0:M_HALF], w_rows[1][:, :, 0:M_HALF])
         nc.sync.dma_start(raw1[:, 0:PAIR, M_HALF:M], w_rows[1][:, 0:PAIR, M_HALF:M])
         for m in range(M_HALF // M_TILE, ROW_TILES):

@@ -102,10 +102,9 @@ def tile_list_tabw_none_kernel(tc, tab, w, offs, out):
         load_scales()
         nc.sync.dma_start(raw0_run[:, M_HALF:], w0_run[:, M_HALF:])
         nc.sync.dma_start(raw1[:, :, 0:M_HALF], w_rows[1][:, :, 0:M_HALF])
-        nc.sync.dma_start(raw1[:, 0:PAIR, M_HALF:M], w_rows[1][:, 0:PAIR, M_HALF:M])
         for m in range(M_HALF // M_TILE, ROW_TILES):
             cols = slice(m * M_TILE, (m + 1) * M_TILE)
-            nc.sync.dma_start(raw1[:, PAIR:PACK, cols], w_rows[1][:, PAIR:PACK, cols])
+            nc.sync.dma_start(raw1[:, :, cols], w_rows[1][:, :, cols])
 
         for a in range(PASSES):
             pick_words(a)

@@ -15,7 +15,6 @@ FP8X4 = mybir.dt.float8_e4m3fn_x4
 
 P = 128
 PACK = 4
-PAIR = 2
 PASSES = K // (P * PACK)
 QUADRANT = 32
 PLANE_ROWS = 4
@@ -24,6 +23,7 @@ M_TILE = 128
 ROW_TILES = M // M_TILE
 M_HALF = M // 2
 S_HALF = S // 2
+HEAD = M - M_TILE
 
 
 def tile_list_tabw_none_kernel(tc, tab, w, offs, out):
@@ -94,27 +94,28 @@ def tile_list_tabw_none_kernel(tc, tab, w, offs, out):
 
         nc.vector.memset(tab_scales[:], 0)
 
-        nc.sync.dma_start(words[:], tab_words[:, 0 : P * T].rearrange("a (p c) -> p a c", p=P))
+        words_hbm = tab_words[:, 0 : P * T].rearrange("a (p c) -> a p c", p=P)
+        nc.sync.dma_start(words[:, 0, :], words_hbm[0])
         nc.sync.dma_start(offsets[:], offs)
         raw0_run = raw0[:].rearrange("p t n -> p (t n)")
         w0_run = w_rows[0].rearrange("p t n -> p (t n)")
-        nc.sync.dma_start(raw0_run[:, 0:M_HALF], w0_run[:, 0:M_HALF])
+        nc.sync.dma_start(raw0_run[:, :HEAD], w0_run[:, :HEAD])
         load_scales()
-        nc.sync.dma_start(raw0_run[:, M_HALF:], w0_run[:, M_HALF:])
+        nc.sync.dma_start(raw0_run[:, HEAD:], w0_run[:, HEAD:])
+        nc.sync.dma_start(words[:, 1, :], words_hbm[1])
         nc.sync.dma_start(raw1[:, :, 0:M_HALF], w_rows[1][:, :, 0:M_HALF])
         for m in range(M_HALF // M_TILE, ROW_TILES):
             cols = slice(m * M_TILE, (m + 1) * M_TILE)
             nc.sync.dma_start(raw1[:, :, cols], w_rows[1][:, :, cols])
 
-        for a in range(PASSES):
-            pick_words(a)
+        pick_words(0)
         for a in range(PASSES):
             pick_scales(a)
 
-        grouped0 = [
-            interleave(copy, raw0, f"g0{m}", f"g0{m}", m) for m, copy in enumerate((vector_copy, vector_copy, scalar_copy, scalar_copy))
-        ]
-        for m in range(ROW_TILES):
+        order0 = ((0, vector_copy), (3, scalar_copy), (2, scalar_copy), (1, scalar_copy))
+        grouped0 = {m: interleave(copy, raw0, f"g0{m}", f"g0{m}", m) for m, copy in order0}
+        pick_words(1)
+        for m, copy in order0:
             quantize_and_multiply(0, grouped0[m], m)
 
         tile0 = interleave(scalar_copy, raw1, "g10", "g10", 0)

@@ -23,7 +23,6 @@ M_TILE = 128
 ROW_TILES = M // M_TILE
 M_HALF = M // 2
 S_HALF = S // 2
-HEAD = M - M_TILE
 
 
 def tile_list_tabw_none_kernel(tc, tab, w, offs, out):
@@ -97,11 +96,9 @@ def tile_list_tabw_none_kernel(tc, tab, w, offs, out):
         words_hbm = tab_words[:, 0 : P * T].rearrange("a (p c) -> a p c", p=P)
         nc.sync.dma_start(words[:, 0, :], words_hbm[0])
         nc.sync.dma_start(offsets[:], offs)
-        raw0_run = raw0[:].rearrange("p t n -> p (t n)")
-        w0_run = w_rows[0].rearrange("p t n -> p (t n)")
-        nc.sync.dma_start(raw0_run[:, :HEAD], w0_run[:, :HEAD])
+        nc.sync.dma_start(raw0[:, :, 0:M_HALF], w_rows[0][:, :, 0:M_HALF])
         load_scales()
-        nc.sync.dma_start(raw0_run[:, HEAD:], w0_run[:, HEAD:])
+        nc.sync.dma_start(raw0[:, :, M_HALF:M], w_rows[0][:, :, M_HALF:M])
         nc.sync.dma_start(words[:, 1, :], words_hbm[1])
         nc.sync.dma_start(raw1[:, :, 0:M_HALF], w_rows[1][:, :, 0:M_HALF])
         for m in range(M_HALF // M_TILE, ROW_TILES):
@@ -112,10 +109,10 @@ def tile_list_tabw_none_kernel(tc, tab, w, offs, out):
         for a in range(PASSES):
             pick_scales(a)
 
-        order0 = ((0, vector_copy), (3, scalar_copy), (2, scalar_copy), (1, scalar_copy))
-        grouped0 = {m: interleave(copy, raw0, f"g0{m}", f"g0{m}", m) for m, copy in order0}
-        pick_words(1)
-        for m, copy in order0:
+        grouped0 = [interleave(scalar_copy, raw0, f"g0{m}", f"g0{m}", m) for m in range(ROW_TILES)]
+        for m in range(ROW_TILES):
+            if m == ROW_TILES // 2:
+                pick_words(1)
             quantize_and_multiply(0, grouped0[m], m)
 
         tile0 = interleave(scalar_copy, raw1, "g10", "g10", 0)

@@ -118,11 +118,11 @@ def tile_list_tabw_none_kernel(tc, tab, w, offs, out):
         tile0 = interleave(scalar_copy, raw1, "g10", "g10", 0)
         tile1 = interleave(vector_copy, raw1, "g11", "raw0", 1)
         tile2 = interleave(scalar_copy, raw1, "g12", "g12", 2)
-        quantize_and_multiply(1, tile0, 0)
         quantize_and_multiply(1, tile1, 1)
-        tile3 = interleave(vector_copy, raw1, "g13", "g10", 3)
+        quantize_and_multiply(1, tile0, 0)
+        tile3 = interleave(vector_copy, raw1, "g13", "raw0", 3)
         quantize_and_multiply(1, tile2, 2)
         quantize_and_multiply(1, tile3, 3)
 
-        for m in range(ROW_TILES):
+        for m in (1, 0, 2, 3):
             store(m)

@@ -42,10 +42,10 @@ def tile_list_tabw_none_kernel(tc, tab, w, offs, out):
         picked = {}
         picked_scales = {}
         sums = {}
-        tab_scales = held.tile([P, PASSES, scale_row], I32, name="tab_scales", align_bytes=64)
-        words = held.tile([P, PASSES, T], I32, name="words", align_bytes=64)
-        raw0 = held.tile([P, PACK, M], F32, name="raw0", tag="raw0", align_bytes=64)
-        raw1 = held.tile([P, PACK, M], F32, name="raw1", align_bytes=64)
+        tab_scales = held.tile([P, PASSES, scale_row], I32, name="tab_scales", align_bytes=256)
+        words = held.tile([P, PASSES, T], I32, name="words", align_bytes=256)
+        raw0 = held.tile([P, PACK, M], F32, name="raw0", tag="raw0", align_bytes=256)
+        raw1 = held.tile([P, PACK, M], F32, name="raw1", align_bytes=256)
 
         def load_scales():
             rows = tab_words[:, P * T :].rearrange("a (q r c) -> r q a c", r=PLANE_ROWS, c=scale_row)
@@ -53,15 +53,15 @@ def tile_list_tabw_none_kernel(tc, tab, w, offs, out):
                 nc.sync.dma_start(tab_scales[r:P:QUADRANT, :, :], rows[r])
 
         def pick_words(a):
-            picked[a] = held.tile([P, S], U32, name=f"picked{a}", align_bytes=64)
+            picked[a] = held.tile([P, S], U32, name=f"picked{a}", align_bytes=256)
             nc.vector.tensor_copy(picked[a][:], words[:, a, :].bitcast(U32).indirect(offsets[:]))
 
         def pick_scales(a):
-            picked_scales[a] = held.tile([P, S], U8, name=f"picked_scales{a}", align_bytes=64)
+            picked_scales[a] = held.tile([P, S], U8, name=f"picked_scales{a}", align_bytes=256)
             nc.vector.tensor_copy(picked_scales[a][:], tab_scales[:, a, :].bitcast(U8).indirect(offsets[:]))
 
         def interleave(copy, raw, name, tag, m):
-            grouped = held.tile([P, M_TILE, PACK], BF16, name=name, tag=tag, align_bytes=64)
+            grouped = held.tile([P, M_TILE, PACK], BF16, name=name, tag=tag, align_bytes=256)
             copy(
                 out=grouped[:].rearrange("p (c i) t -> p c t i", i=LINE),
                 in_=raw[:, :, m * M_TILE : (m + 1) * M_TILE].rearrange("p t (c i) -> p c t i", i=LINE),
@@ -69,8 +69,8 @@ def tile_list_tabw_none_kernel(tc, tab, w, offs, out):
             return grouped
 
         def quantize_and_multiply(a, grouped, m):
-            codes = held.tile([P, M_TILE], U32, name=f"codes{a}_{m}", align_bytes=64)
-            plane = held.tile([P, M_TILE], U8, name=f"plane{a}_{m}", align_bytes=64)
+            codes = held.tile([P, M_TILE], U32, name=f"codes{a}_{m}", align_bytes=256)
+            plane = held.tile([P, M_TILE], U8, name=f"plane{a}_{m}", align_bytes=256)
             nc.vector.quantize_mx(out=codes[:].bitcast(FP8X4), scales=plane[:], in_=grouped[:].rearrange("p c t -> p (c t)"))
             for begin, end, copy in parts[m]:
                 if a == 0:
@@ -86,7 +86,7 @@ def tile_list_tabw_none_kernel(tc, tab, w, offs, out):
                 )
 
         def store(m):
-            result = held.tile([M_TILE, S], F32, name=f"result{m}", align_bytes=64)
+            result = held.tile([M_TILE, S], F32, name=f"result{m}", align_bytes=256)
             for begin, end, copy in parts[m]:
                 copy(out=result[:, begin:end], in_=sums[m, begin][:])
             nc.sync.dma_start(out=out[m * M_TILE : (m + 1) * M_TILE, 0:S], in_=result[:, 0:S])

@@ -28,9 +28,7 @@ S_HALF = S // 2
 def tile_list_tabw_none_kernel(tc, tab, w, offs, out):
     nc = tc.nc
     vector_copy, scalar_copy = nc.vector.tensor_copy, nc.scalar.copy
-    by_scalar = ((0, S_HALF, scalar_copy), (S_HALF, S, scalar_copy))
-    by_both = ((0, S_HALF, vector_copy), (S_HALF, S, scalar_copy))
-    parts = (by_scalar, by_scalar, by_both, by_both)
+    halves = ((0, S_HALF), (S_HALF, S))
     with ExitStack() as ctx:
         held = ctx.enter_context(tc.tile_pool(name="held", bufs=1))
         psum = ctx.enter_context(tc.psum_pool(name="psum", bufs=1))
@@ -39,90 +37,123 @@ def tile_list_tabw_none_kernel(tc, tab, w, offs, out):
         tab_words = tab.bitcast(I32)
         scale_row = T // 4
         w_rows = w.rearrange("(a p t) n -> a p t n", p=P, t=PACK)
-        picked = {}
-        picked_scales = {}
-        sums = {}
         tab_scales = held.tile([P, PASSES, scale_row], I32, name="tab_scales", align_bytes=256)
         words = held.tile([P, PASSES, T], I32, name="words", align_bytes=256)
-        raw0 = held.tile([P, PACK, M], F32, name="raw0", tag="raw0", align_bytes=256)
-        raw1 = held.tile([P, PACK, M], F32, name="raw1", align_bytes=256)
+        raw = {}
+        picked = [held.tile([P, S], U32, name=f"picked{a}", align_bytes=256) for a in range(PASSES)]
+        picked_scales = [held.tile([P, S], U8, name=f"picked_scales{a}", align_bytes=256) for a in range(PASSES)]
+        codes, planes, sums, results = {}, {}, {}, {}
 
-        def load_scales():
-            rows = tab_words[:, P * T :].rearrange("a (q r c) -> r q a c", r=PLANE_ROWS, c=scale_row)
-            for r in range(PLANE_ROWS):
-                nc.sync.dma_start(tab_scales[r:P:QUADRANT, :, :], rows[r])
+        def load_w(a, first, count):
+            name = f"raw{a}_{first}"
+            loaded = held.tile([P, PACK, M], F32, name=name, tag=name, align_bytes=256)
+            columns = slice(first * M_TILE, (first + count) * M_TILE)
+            nc.sync.dma_start(loaded[:, :, columns], w_rows[a][:, :, columns])
+            for m in range(first, first + count):
+                raw[a, m] = loaded[:, :, m * M_TILE : (m + 1) * M_TILE]
 
-        def pick_words(a):
-            picked[a] = held.tile([P, S], U32, name=f"picked{a}", align_bytes=256)
-            nc.vector.tensor_copy(picked[a][:], words[:, a, :].bitcast(U32).indirect(offsets[:]))
+        def new_grouped(a, m, tag=None):
+            name = f"grouped{a}_{m}"
+            return held.tile([P, M_TILE, PACK], BF16, name=name, tag=tag or name, align_bytes=256)
 
-        def pick_scales(a):
-            picked_scales[a] = held.tile([P, S], U8, name=f"picked_scales{a}", align_bytes=256)
-            nc.vector.tensor_copy(picked_scales[a][:], tab_scales[:, a, :].bitcast(U8).indirect(offsets[:]))
-
-        def interleave(copy, raw, name, tag, m):
-            grouped = held.tile([P, M_TILE, PACK], BF16, name=name, tag=tag, align_bytes=256)
+        def interleave(copy, grouped, a, m, begin=0, end=M_TILE):
             copy(
-                out=grouped[:].rearrange("p (c i) t -> p c t i", i=LINE),
-                in_=raw[:, :, m * M_TILE : (m + 1) * M_TILE].rearrange("p t (c i) -> p c t i", i=LINE),
+                out=grouped[:, begin:end, :].rearrange("p (c i) t -> p c t i", i=LINE),
+                in_=raw[a, m][:, :, begin:end].rearrange("p t (c i) -> p c t i", i=LINE),
             )
-            return grouped
 
-        def quantize_and_multiply(a, grouped, m):
-            codes = held.tile([P, M_TILE], U32, name=f"codes{a}_{m}", align_bytes=256)
-            plane = held.tile([P, M_TILE], U8, name=f"plane{a}_{m}", align_bytes=256)
-            nc.vector.quantize_mx(out=codes[:].bitcast(FP8X4), scales=plane[:], in_=grouped[:].rearrange("p c t -> p (c t)"))
-            for begin, end, copy in parts[m]:
+        def quantize(grouped, a, m, begin=0, end=M_TILE, tag=None):
+            if (a, m) not in codes:
+                codes[a, m] = held.tile([P, M_TILE], U32, name=f"codes{a}_{m}", tag=tag or f"codes{a}_{m}", align_bytes=256)
+                planes[a, m] = held.tile([P, M_TILE], U8, name=f"plane{a}_{m}", align_bytes=256)
+            nc.vector.quantize_mx(
+                out=codes[a, m][:, begin:end].bitcast(FP8X4),
+                scales=planes[a, m][:, begin:end],
+                in_=grouped[:, begin:end, :].rearrange("p c t -> p (c t)"),
+            )
+
+        def multiply(a, m):
+            for begin, end in halves:
                 if a == 0:
-                    sums[m, begin] = psum.tile([M_TILE, end - begin], F32, name=f"sum{m}_{begin}")
+                    sums[m, begin] = psum.tile([M_TILE, S_HALF], F32, name=f"sum{m}_{begin}")
                 nc.tensor.matmul_mx(
                     out=sums[m, begin][:],
-                    lhsT=codes[:].bitcast(FP8X4),
-                    lhsT_scale=plane[:],
+                    lhsT=codes[a, m][:].bitcast(FP8X4),
+                    lhsT_scale=planes[a, m][:],
                     rhs=picked[a][:, begin:end].bitcast(FP8X4),
                     rhs_scale=picked_scales[a][:, begin:end],
                     start=(a == 0),
                     stop=(a == PASSES - 1),
                 )
 
-        def store(m):
-            result = held.tile([M_TILE, S], F32, name=f"result{m}", align_bytes=256)
-            for begin, end, copy in parts[m]:
-                copy(out=result[:, begin:end], in_=sums[m, begin][:])
-            nc.sync.dma_start(out=out[m * M_TILE : (m + 1) * M_TILE, 0:S], in_=result[:, 0:S])
+        def copy_out(copy, m, begin, end):
+            if m not in results:
+                results[m] = held.tile([M_TILE, S], F32, name=f"result{m}", align_bytes=256)
+            copy(out=results[m][:, begin:end], in_=sums[m, begin][:])
+
+        def store(m, begin=0, end=S):
+            nc.sync.dma_start(out=out[m * M_TILE : (m + 1) * M_TILE, begin:end], in_=results[m][:, begin:end])
 
         nc.vector.memset(tab_scales[:], 0)
 
         words_hbm = tab_words[:, 0 : P * T].rearrange("a (p c) -> a p c", p=P)
         nc.sync.dma_start(words[:, 0, :], words_hbm[0])
         nc.sync.dma_start(offsets[:], offs)
-        nc.sync.dma_start(raw0[:, :, 0:M_HALF], w_rows[0][:, :, 0:M_HALF])
-        load_scales()
-        nc.sync.dma_start(raw0[:, :, M_HALF:M], w_rows[0][:, :, M_HALF:M])
+        load_w(0, 0, 2)
+        rows = tab_words[:, P * T :].rearrange("a (q r c) -> r q a c", r=PLANE_ROWS, c=scale_row)
+        for r in range(PLANE_ROWS):
+            nc.sync.dma_start(tab_scales[r:P:QUADRANT, :, :], rows[r])
+        load_w(1, 0, 2)
         nc.sync.dma_start(words[:, 1, :], words_hbm[1])
-        nc.sync.dma_start(raw1[:, :, 0:M_HALF], w_rows[1][:, :, 0:M_HALF])
-        for m in range(M_HALF // M_TILE, ROW_TILES):
-            cols = slice(m * M_TILE, (m + 1) * M_TILE)
-            nc.sync.dma_start(raw1[:, :, cols], w_rows[1][:, :, cols])
+        load_w(0, 2, 2)
+        load_w(1, 2, 1)
+        load_w(1, 3, 1)
 
-        pick_words(0)
+        vector_copy(picked[0][:], words[:, 0, :].bitcast(U32).indirect(offsets[:]))
         for a in range(PASSES):
-            pick_scales(a)
+            vector_copy(picked_scales[a][:], tab_scales[:, a, :].bitcast(U8).indirect(offsets[:]))
 
-        grouped0 = [interleave(scalar_copy, raw0, f"g0{m}", f"g0{m}", m) for m in range(ROW_TILES)]
-        for m in range(ROW_TILES):
-            if m == ROW_TILES // 2:
-                pick_words(1)
-            quantize_and_multiply(0, grouped0[m], m)
+        for m in range(2):
+            grouped = new_grouped(0, m)
+            interleave(scalar_copy, grouped, 0, m)
+            quantize(grouped, 0, m)
+            multiply(0, m)
+        vector_copy(picked[1][:], words[:, 1, :].bitcast(U32).indirect(offsets[:]))
+        g10, g11 = new_grouped(1, 0), new_grouped(1, 1)
+        interleave(scalar_copy, g10, 1, 0)
+        interleave(scalar_copy, g11, 1, 1)
+        for m, g in ((0, g10), (1, g11)):
+            quantize(g, 1, m)
+            multiply(1, m)
 
-        tile0 = interleave(scalar_copy, raw1, "g10", "g10", 0)
-        tile1 = interleave(vector_copy, raw1, "g11", "raw0", 1)
-        tile2 = interleave(scalar_copy, raw1, "g12", "g12", 2)
-        quantize_and_multiply(1, tile1, 1)
-        quantize_and_multiply(1, tile0, 0)
-        tile3 = interleave(vector_copy, raw1, "g13", "raw0", 3)
-        quantize_and_multiply(1, tile2, 2)
-        quantize_and_multiply(1, tile3, 3)
+        g02, g03 = new_grouped(0, 2), new_grouped(0, 3, "raw1_0")
+        interleave(scalar_copy, g02, 0, 2)
+        interleave(vector_copy, g03, 0, 3)
+        for m, g in ((3, g03), (2, g02)):
+            quantize(g, 0, m)
+            multiply(0, m)
+        results[0] = held.tile([M_TILE, S], F32, name="result0", tag="raw0_2", align_bytes=256)
+        for begin, end in halves:
+            copy_out(vector_copy, 0, begin, end)
+        store(0)
 
-        for m in (1, 0, 2, 3):
-            store(m)
+        g12, g13 = new_grouped(1, 2), new_grouped(1, 3, "raw1_0")
+        half = M_TILE // 2
+        interleave(scalar_copy, g12, 1, 2)
+        interleave(vector_copy, g13, 1, 3, 0, half)
+        interleave(scalar_copy, g13, 1, 3, half, M_TILE)
+        quantize(g12, 1, 2)
+        multiply(1, 2)
+        quantize(g13, 1, 3, half, M_TILE)
+        quantize(g13, 1, 3, 0, half)
+        multiply(1, 3)
+        results[1] = held.tile([M_TILE, S], F32, name="result1", tag="raw1_3", align_bytes=256)
+        for begin, end in halves:
+            copy_out(scalar_copy, 1, begin, end)
+        store(1)
+        for copy, (begin, end) in zip((vector_copy, scalar_copy), halves):
+            copy_out(copy, 2, begin, end)
+        store(2)
+        for copy, (begin, end) in zip((vector_copy, scalar_copy), halves):
+            copy_out(copy, 3, begin, end)
+        store(3)

@@ -127,8 +127,10 @@ def tile_list_tabw_none_kernel(tc, tab, w, offs, out):
             multiply(1, m)
 
         g02, g03 = new_grouped(0, 2), new_grouped(0, 3, "raw1_0")
-        interleave(scalar_copy, g02, 0, 2)
+        half = M_TILE // 2
+        interleave(scalar_copy, g02, 0, 2, half, M_TILE)
         interleave(vector_copy, g03, 0, 3)
+        interleave(vector_copy, g02, 0, 2, 0, half)
         for m, g in ((3, g03), (2, g02)):
             quantize(g, 0, m)
             multiply(0, m)
@@ -138,7 +140,6 @@ def tile_list_tabw_none_kernel(tc, tab, w, offs, out):
         store(0)
 
         g12, g13 = new_grouped(1, 2), new_grouped(1, 3, "raw1_0")
-        half = M_TILE // 2
         interleave(scalar_copy, g12, 1, 2)
         interleave(vector_copy, g13, 1, 3, 0, half)
         interleave(scalar_copy, g13, 1, 3, half, M_TILE)

@@ -126,7 +126,7 @@ def tile_list_tabw_none_kernel(tc, tab, w, offs, out):
             quantize(g, 1, m)
             multiply(1, m)
 
-        g02, g03 = new_grouped(0, 2), new_grouped(0, 3, "raw1_0")
+        g02, g03 = new_grouped(0, 2), new_grouped(0, 3)
         half = M_TILE // 2
         interleave(scalar_copy, g02, 0, 2, half, M_TILE)
         interleave(vector_copy, g03, 0, 3)
@@ -139,7 +139,7 @@ def tile_list_tabw_none_kernel(tc, tab, w, offs, out):
             copy_out(vector_copy, 0, begin, end)
         store(0)
 
-        g12, g13 = new_grouped(1, 2), new_grouped(1, 3, "raw1_0")
+        g12, g13 = new_grouped(1, 2), new_grouped(1, 3)
         interleave(scalar_copy, g12, 1, 2)
         interleave(vector_copy, g13, 1, 3, 0, half)
         interleave(scalar_copy, g13, 1, 3, half, M_TILE)

from contextlib import ExitStack

import concourse.mybir as mybir

K, M, T, S = 1024, 512, 512, 256
FLOPS = 2 * K * M * S

F32 = mybir.dt.float32
BF16 = mybir.dt.bfloat16
I32 = mybir.dt.int32
U32 = mybir.dt.uint32
U16 = mybir.dt.uint16
U8 = mybir.dt.uint8
FP8X4 = mybir.dt.float8_e4m3fn_x4

P = 128
PACK = 4
PASSES = K // (P * PACK)
QUADRANT = 32
PLANE_ROWS = 4
LINE = 4
M_TILE = 128
ROW_TILES = M // M_TILE
M_HALF = M // 2
S_HALF = S // 2


def tile_list_tabw_none_kernel(tc, tab, w, offs, out):
    nc = tc.nc
    vector_copy, scalar_copy = nc.vector.tensor_copy, nc.scalar.copy
    halves = ((0, S_HALF), (S_HALF, S))
    with ExitStack() as ctx:
        held = ctx.enter_context(tc.tile_pool(name="held", bufs=1))
        psum = ctx.enter_context(tc.psum_pool(name="psum", bufs=1))

        offsets = held.tile([P, S // 16], U16, name="offsets")
        tab_words = tab.bitcast(I32)
        scale_row = T // 4
        w_rows = w.rearrange("(a p t) n -> a p t n", p=P, t=PACK)
        tab_scales = held.tile([P, PASSES, scale_row], I32, name="tab_scales", align_bytes=256)
        words = held.tile([P, PASSES, T], I32, name="words", align_bytes=256)
        raw = {}
        picked = [held.tile([P, S], U32, name=f"picked{a}", align_bytes=256) for a in range(PASSES)]
        picked_scales = [held.tile([P, S], U8, name=f"picked_scales{a}", align_bytes=256) for a in range(PASSES)]
        codes, planes, sums, results = {}, {}, {}, {}

        def load_w(a, first, count):
            name = f"raw{a}_{first}"
            loaded = held.tile([P, PACK, M], F32, name=name, tag=name, align_bytes=256)
            columns = slice(first * M_TILE, (first + count) * M_TILE)
            nc.sync.dma_start(loaded[:, :, columns], w_rows[a][:, :, columns])
            for m in range(first, first + count):
                raw[a, m] = loaded[:, :, m * M_TILE : (m + 1) * M_TILE]

        def new_grouped(a, m, tag=None):
            name = f"grouped{a}_{m}"
            return held.tile([P, M_TILE, PACK], BF16, name=name, tag=tag or name, align_bytes=256)

        def interleave(copy, grouped, a, m, begin=0, end=M_TILE):
            copy(
                out=grouped[:, begin:end, :].rearrange("p (c i) t -> p c t i", i=LINE),
                in_=raw[a, m][:, :, begin:end].rearrange("p t (c i) -> p c t i", i=LINE),
            )

        def quantize(grouped, a, m, begin=0, end=M_TILE, tag=None):
            if (a, m) not in codes:
                codes[a, m] = held.tile([P, M_TILE], U32, name=f"codes{a}_{m}", tag=tag or f"codes{a}_{m}", align_bytes=256)
                planes[a, m] = held.tile([P, M_TILE], U8, name=f"plane{a}_{m}", align_bytes=256)
            nc.vector.quantize_mx(
                out=codes[a, m][:, begin:end].bitcast(FP8X4),
                scales=planes[a, m][:, begin:end],
                in_=grouped[:, begin:end, :].rearrange("p c t -> p (c t)"),
            )

        def multiply(a, m):
            for begin, end in halves:
                if a == 0:
                    sums[m, begin] = psum.tile([M_TILE, S_HALF], F32, name=f"sum{m}_{begin}")
                nc.tensor.matmul_mx(
                    out=sums[m, begin][:],
                    lhsT=codes[a, m][:].bitcast(FP8X4),
                    lhsT_scale=planes[a, m][:],
                    rhs=picked[a][:, begin:end].bitcast(FP8X4),
                    rhs_scale=picked_scales[a][:, begin:end],
                    start=(a == 0),
                    stop=(a == PASSES - 1),
                )

        def copy_out(copy, m, begin, end):
            if m not in results:
                results[m] = held.tile([M_TILE, S], F32, name=f"result{m}", align_bytes=256)
            copy(out=results[m][:, begin:end], in_=sums[m, begin][:])

        def store(m, begin=0, end=S):
            nc.sync.dma_start(out=out[m * M_TILE : (m + 1) * M_TILE, begin:end], in_=results[m][:, begin:end])

        nc.vector.memset(tab_scales[:], 0)

        words_hbm = tab_words[:, 0 : P * T].rearrange("a (p c) -> a p c", p=P)
        nc.sync.dma_start(words[:, 0, :], words_hbm[0])
        nc.sync.dma_start(offsets[:], offs)
        load_w(0, 0, 2)
        rows = tab_words[:, P * T :].rearrange("a (q r c) -> r q a c", r=PLANE_ROWS, c=scale_row)
        for r in range(PLANE_ROWS):
            nc.sync.dma_start(tab_scales[r:P:QUADRANT, :, :], rows[r])
        load_w(1, 0, 2)
        nc.sync.dma_start(words[:, 1, :], words_hbm[1])
        load_w(0, 2, 2)
        load_w(1, 2, 1)
        load_w(1, 3, 1)

        vector_copy(picked[0][:], words[:, 0, :].bitcast(U32).indirect(offsets[:]))
        for a in range(PASSES):
            vector_copy(picked_scales[a][:], tab_scales[:, a, :].bitcast(U8).indirect(offsets[:]))

        for m in range(2):
            grouped = new_grouped(0, m)
            interleave(scalar_copy, grouped, 0, m)
            quantize(grouped, 0, m)
            multiply(0, m)
        vector_copy(picked[1][:], words[:, 1, :].bitcast(U32).indirect(offsets[:]))
        g10, g11 = new_grouped(1, 0), new_grouped(1, 1)
        interleave(scalar_copy, g10, 1, 0)
        interleave(scalar_copy, g11, 1, 1)
        for m, g in ((0, g10), (1, g11)):
            quantize(g, 1, m)
            multiply(1, m)

        g02, g03 = new_grouped(0, 2), new_grouped(0, 3)
        half = M_TILE // 2
        interleave(scalar_copy, g02, 0, 2, half, M_TILE)
        interleave(vector_copy, g03, 0, 3)
        interleave(vector_copy, g02, 0, 2, 0, half)
        for m, g in ((3, g03), (2, g02)):
            quantize(g, 0, m)
            multiply(0, m)
        results[0] = held.tile([M_TILE, S], F32, name="result0", tag="raw0_2", align_bytes=256)
        for begin, end in halves:
            copy_out(vector_copy, 0, begin, end)
        store(0)

        g12, g13 = new_grouped(1, 2), new_grouped(1, 3)
        interleave(scalar_copy, g12, 1, 2)
        interleave(vector_copy, g13, 1, 3, 0, half)
        interleave(scalar_copy, g13, 1, 3, half, M_TILE)
        quantize(g12, 1, 2)
        multiply(1, 2)
        quantize(g13, 1, 3, half, M_TILE)
        quantize(g13, 1, 3, 0, half)
        multiply(1, 3)
        results[1] = held.tile([M_TILE, S], F32, name="result1", tag="raw1_3", align_bytes=256)
        for begin, end in halves:
            copy_out(scalar_copy, 1, begin, end)
        store(1)
        for copy, (begin, end) in zip((vector_copy, scalar_copy), halves):
            copy_out(copy, 2, begin, end)
        store(2)
        for copy, (begin, end) in zip((vector_copy, scalar_copy), halves):
            copy_out(copy, 3, begin, end)
        store(3)
